import numpy as np
import ml_dtypes


def mxq(x, axis, fmt="e4m3"):
    dtype, down = {"e4m3": (ml_dtypes.float8_e4m3fn, 7), "e5m2": (ml_dtypes.float8_e5m2, 14)}[fmt]
    v = np.moveaxis(np.asarray(x, np.float32).astype(ml_dtypes.bfloat16).astype(np.float64), axis, -1)
    blocks = v.reshape(v.shape[:-1] + (-1, 32))
    amax = np.abs(blocks).max(-1, keepdims=True)
    byte = np.maximum(np.where(amax > 0, np.frexp(amax)[1] - 1 + 127, 0) - down, 1)
    scale = np.exp2(byte - 127.0)
    codes = (blocks / scale).astype(np.float32).astype(dtype).astype(np.float64)
    return np.moveaxis((codes * scale).reshape(v.shape), -1, axis)


WIDE = False


def mx_kscale(k):
    if not WIDE:
        return np.ones(k)
    levels = np.array([18, -18])
    if k % 512:
        return np.exp2(np.random.permutation(np.resize(levels, k // 32))).repeat(32)
    a = np.empty((k // 512, 16))
    for p in range(k // 512):
        a[p, :8] = np.random.permutation(np.resize(levels, 8))
        for g in range(8):
            far = levels[np.abs(levels - a[p, g]) >= 10]
            a[p, g + 8] = far[np.random.randint(len(far))]
    return np.exp2(a.ravel()).repeat(32)


def f64(x):
    return np.asarray(x).astype(np.float64)


def striped(idx):
    return np.tile(np.asarray(idx).reshape(-1, 16).T, (8, 1)).astype(np.uint16)


def unstriped(offs):
    return offs[:16].T.reshape(-1).astype(np.int64)

def planes(y):
    n, m = y.shape
    v = y.astype(np.float32).astype(ml_dtypes.bfloat16).astype(np.float64).reshape(n // 32, 32, m)
    top = np.abs(v).max(1)
    byte = np.clip(np.where(top > 0, np.frexp(top)[1] - 1 + 127 - 7, 1), 1, 254)
    codes = (v * np.exp2(127.0 - byte)[:, None, :]).reshape(n, m).astype(np.float32).astype(ml_dtypes.float8_e4m3fn).view(np.uint8)
    words = codes.reshape(n // 512, 128, 4, m).transpose(0, 1, 3, 2)
    return np.ascontiguousarray(words), np.ascontiguousarray(byte.astype(np.uint8).reshape(n // 512, 16, m))


T, C, D, DV = 1024, 512, 512, 512
BETA = 0.25


def setup_inputs():
    n = np.random.standard_normal
    grid = lambda v: np.clip(np.round(v * 16) / 16, -4, 4)
    v = mx_kscale(DV)[:, None]
    return {
        "zT": (grid(n((DV, T))) * v).astype(np.float32),
        "cb": (grid(n((DV, C))) * v).astype(np.float32),
        "cb2": (grid(0.5 * n((DV, C))) * v).astype(np.float32),
        "dyT": (grid(0.5 * n((DV, T))) * v).astype(np.float32),
        "wm": (n((DV, D)) / np.sqrt(DV) / v).astype(np.float32),
        "offs": striped(np.random.randint(0, C, T)),
        "offs2": striped(np.random.randint(0, C, T)),
    }


def reference(zT, cb, cb2, dyT, wm, offs, offs2):
    e = f64(zT) - f64(cb)[:, unstriped(offs)] - f64(cb2)[:, unstriped(offs2)]
    g = (f64(dyT) + BETA * e)
    out_0 = mxq(f64(wm), 0, "e4m3").T @ mxq(g, 0, "e5m2")
    return (out_0,) + planes(out_0)

@@ -1,0 +1,189 @@
+from contextlib import ExitStack
+
+import concourse.mybir as mybir
+
+T, C, D, DV = 1024, 512, 512, 512
+BETA = 0.25
+FLOPS = 2 * T * D * DV
+
+F32 = mybir.dt.float32
+BF16 = mybir.dt.bfloat16
+I32 = mybir.dt.int32
+U32 = mybir.dt.uint32
+U16 = mybir.dt.uint16
+U8 = mybir.dt.uint8
+E4M3 = mybir.dt.float8_e4m3fn_x4
+E5M2 = mybir.dt.float8_e5m2_x4
+ADD = mybir.AluOpType.add
+SUB = mybir.AluOpType.subtract
+MULT = mybir.AluOpType.mult
+
+P = 128
+PACK = 4
+HALF = 512
+CHUNK = 256
+GROUP = 16
+
+
+def tile_attend_gvq_pl_rs_x_kernel(tc, zT, cb, cb2, dyT, wm, offs, offs2, out_0, out_1, out_2):
+    nc = tc.nc
+    z_rows = zT.rearrange("(p j) t -> p j t", j=PACK)
+    dy_rows = dyT.rearrange("(p j) t -> p j t", j=PACK)
+    cb_rows = cb.rearrange("(p j) c -> p j c", j=PACK)
+    cb2_rows = cb2.rearrange("(p j) c -> p j c", j=PACK)
+    y_rows = out_0.rearrange("(p j) t -> p j t", j=PACK)
+    word_rows = out_1[0].rearrange("p t l -> p (t l)").bitcast(I32)
+    scale_rows = out_2[0].bitcast(I32)
+
+    with ExitStack() as ctx:
+        keep = ctx.enter_context(tc.tile_pool(name="keep", bufs=1))
+        psum = ctx.enter_context(tc.psum_pool(name="psum", bufs=1))
+
+        code1 = keep.tile([P, T // GROUP], U16, name="code1")
+        code2 = keep.tile([P, T // GROUP], U16, name="code2")
+        book1 = [keep.tile([P, C], F32, name="book1_%d" % j) for j in range(PACK)]
+        book2 = [keep.tile([P, C], F32, name="book2_%d" % j) for j in range(PACK)]
+        z = [[keep.tile([P, HALF], F32, name="z_%d_%d" % (h, j)) for j in range(PACK)] for h in range(2)]
+        dy = [[keep.tile([P, 2, HALF], F32, name="dy_%d_%d" % (h, u)) for u in range(2)] for h in range(2)]
+        w_raw = keep.tile([P, PACK, D], F32, name="w_raw")
+
+        def tokens(h):
+            return slice(h * HALF, (h + 1) * HALF)
+
+        nc.sync.dma_start(code1[:], offs)
+        for j in range(PACK):
+            nc.sync.dma_start(book1[j][:], cb_rows[:, j, :])
+            nc.sync.dma_start(z[0][j][:], z_rows[:, j, tokens(0)])
+            if j == 0:
+                nc.sync.dma_start(code2[:], offs2)
+            nc.sync.dma_start(book2[j][:], cb2_rows[:, j, :])
+            if j % 2 == 1:
+                nc.sync.dma_start(dy[0][j // 2][:], dy_rows[:, j - 1 : j + 1, tokens(0)])
+        for j in range(PACK):
+            nc.sync.dma_start(z[1][j][:], z_rows[:, j, tokens(1)])
+        nc.sync.dma_start(w_raw[:], wm.rearrange("(p j) d -> p j d", j=PACK))
+        for u in range(2):
+            nc.sync.dma_start(dy[1][u][:], dy_rows[:, 2 * u : 2 * u + 2, tokens(1)])
+
+        part = [[keep.tile([P, HALF], F32, name="part_%d_%d" % (h, j)) for j in range(PACK)] for h in range(2)]
+        neg_e = [[keep.tile([P, 2, HALF], F32, name="neg_e_%d_%d" % (h, u)) for u in range(2)] for h in range(2)]
+        g_pairs = [[keep.tile([P, 2, CHUNK * 2], BF16, name="g_pairs_%d_%d" % (h, c)) for c in range(2)] for h in range(2)]
+        g_in = [[keep.tile([P, CHUNK * PACK], BF16, name="g_in_%d_%d" % (h, c), align_bytes=64) for c in range(2)] for h in range(2)]
+        g_codes = [keep.tile([P, HALF], U32, name="g_codes_%d" % h, align_bytes=64) for h in range(2)]
+        g_scales = [keep.tile([P, HALF], U8, name="g_scales_%d" % h, align_bytes=64) for h in range(2)]
+        w_in = keep.tile([P, PACK * D], BF16, name="w_in", align_bytes=64)
+        w_codes = keep.tile([P, D], U32, name="w_codes", align_bytes=64)
+        w_scales = keep.tile([P, D], U8, name="w_scales", align_bytes=64)
+        y = [keep.tile([P, PACK, HALF], F32, name="y_%d" % h) for h in range(2)]
+        y_in = [keep.tile([P, HALF * PACK], BF16, name="y_in_%d" % h, align_bytes=64) for h in range(2)]
+        y_codes = keep.tile([P, T], U32, name="y_codes", align_bytes=64)
+        y_scales = keep.tile([P, T], U8, name="y_scales", align_bytes=64)
+
+        def offsets(code, h, c):
+            first = (h * HALF + c * CHUNK) // GROUP
+            return code[:, first : first + CHUNK // GROUP]
+
+        def look_up_1(h, j, c):
+            cols = slice(c * CHUNK, (c + 1) * CHUNK)
+            nc.vector.tensor_tensor(part[h][j][:, cols], book1[j][:].indirect(offsets(code1, h, c)), z[h][j][:, cols], SUB)
+
+        def look_up_2(h, j, c):
+            cols = slice(c * CHUNK, (c + 1) * CHUNK)
+            nc.vector.tensor_tensor(neg_e[h][j // 2][:, j % 2, cols], book2[j][:].indirect(offsets(code2, h, c)), part[h][j][:, cols], ADD)
+
+        def form_g(h, u, c):
+            cols = slice(c * CHUNK, (c + 1) * CHUNK)
+            nc.vector.scalar_tensor_tensor(
+                g_pairs[h][c][:, u, :].rearrange("p (t e) -> p t e", e=2),
+                neg_e[h][u][:, :, cols].rearrange("p e t -> p t e"),
+                -BETA,
+                dy[h][u][:, :, cols].rearrange("p e t -> p t e"),
+                MULT,
+                ADD,
+            )
+
+        def weave_g(h, c):
+            nc.scalar.copy(
+                g_in[h][c][:].bitcast(F32).rearrange("p (t u) -> p t u", u=2),
+                g_pairs[h][c][:].bitcast(F32).rearrange("p u t -> p t u"),
+            )
+
+        def quantise_g(h, c):
+            cols = slice(c * CHUNK, (c + 1) * CHUNK)
+            nc.vector.quantize_mx(g_codes[h][:, cols].bitcast(E5M2), g_scales[h][:, cols], g_in[h][c][:])
+
+        def multiply(h):
+            banks = []
+            for j in range(PACK):
+                bank = psum.tile([P, HALF], F32, name="bank_%d_%d" % (h, j))
+                cols = slice(j * P, (j + 1) * P)
+                nc.tensor.matmul_mx(bank[:], lhsT=w_codes[:, cols].bitcast(E4M3), lhsT_scale=w_scales[:, cols],
+                                    rhs=g_codes[h][:].bitcast(E5M2), rhs_scale=g_scales[h][:], start=True, stop=True)
+                banks.append(bank)
+            return banks
+
+        def weave_y(engine_copy, h, first, last):
+            engine_copy(
+                y_in[h][:, first * PACK : last * PACK].rearrange("p (c i j) -> p c j i", i=4, j=PACK),
+                y[h][:, :, first:last].rearrange("p j (c i) -> p c j i", i=4),
+            )
+
+        def quantise_y(h):
+            nc.vector.quantize_mx(y_codes[:, tokens(h)].bitcast(E4M3), y_scales[:, tokens(h)], y_in[h][:])
+            nc.sync.dma_start(word_rows[:, tokens(h)], y_codes[:, tokens(h)].bitcast(I32))
+
+        for j in range(PACK):
+            for c in range(2):
+                look_up_1(0, j, c)
+            for c in range(2):
+                look_up_2(0, j, c)
+            if j % 2 == 1:
+                for c in range(2):
+                    form_g(0, j // 2, c)
+        for c in range(2):
+            weave_g(0, c)
+        nc.scalar.copy(
+            w_in[:].rearrange("p (i m j) -> p m j i", i=PACK, j=PACK),
+            w_raw[:].rearrange("p j (m i) -> p m j i", i=PACK),
+        )
+
+        for j in range(PACK):
+            look_up_1(1, j, 0)
+        for c in range(2):
+            quantise_g(0, c)
+        nc.vector.quantize_mx(w_codes[:].bitcast(E4M3), w_scales[:], w_in[:])
+        banks = multiply(0)
+        for j in range(PACK):
+            nc.scalar.copy(y[0][:, j, :], banks[j][:])
+        nc.sync.dma_start(y_rows[:, :, tokens(0)], y[0][:])
+        weave_y(nc.scalar.copy, 0, 0, HALF)
+        for j in range(PACK):
+            look_up_2(1, j, 0)
+        for j in range(PACK):
+            look_up_1(1, j, 1)
+            if j % 2 == 1:
+                form_g(1, j // 2, 0)
+        weave_g(1, 0)
+        for j in range(PACK):
+            look_up_2(1, j, 1)
+            if j == 1:
+                quantise_g(1, 0)
+                quantise_y(0)
+            if j == 2:
+                form_g(1, 0, 1)
+        form_g(1, 1, 1)
+        weave_g(1, 1)
+        quantise_g(1, 1)
+        banks = multiply(1)
+        for j in range(PACK):
+            if j % 2 == 0:
+                nc.scalar.copy(y[1][:, j, :], banks[j][:])
+            else:
+                nc.vector.tensor_copy(y[1][:, j, :], banks[j][:])
+                nc.sync.dma_start(y_rows[:, j - 1 : j + 1, tokens(1)], y[1][:, j - 1 : j + 1, :])
+        weave_y(nc.scalar.copy, 1, 0, 160)
+        weave_y(nc.vector.tensor_copy, 1, 160, HALF)
+        quantise_y(1)
+        for q in range(4):
+            engine = nc.scalar if q % 2 == 0 else nc.sync
+            engine.dma_start(scale_rows[4 * q : 4 * q + 4, :], y_scales[32 * q : 32 * q + 4, :].bitcast(I32))

@@ -1,6 +1,7 @@
 from contextlib import ExitStack
 
 import concourse.mybir as mybir
+from concourse.masks import make_identity
 
 T, C, D, DV = 1024, 512, 512, 512
 BETA = 0.25
@@ -17,6 +18,7 @@ E5M2 = mybir.dt.float8_e5m2_x4
 ADD = mybir.AluOpType.add
 SUB = mybir.AluOpType.subtract
 MULT = mybir.AluOpType.mult
+COPY = mybir.ActivationFunctionType.Copy
 
 P = 128
 PACK = 4
@@ -43,147 +45,251 @@ def tile_attend_gvq_pl_rs_x_kernel(tc, zT, cb, cb2, dyT, wm, offs, offs2, out_0,
         code2 = keep.tile([P, T // GROUP], U16, name="code2")
         book1 = [keep.tile([P, C], F32, name="book1_%d" % j) for j in range(PACK)]
         book2 = [keep.tile([P, C], F32, name="book2_%d" % j) for j in range(PACK)]
-        z = [[keep.tile([P, HALF], F32, name="z_%d_%d" % (h, j)) for j in range(PACK)] for h in range(2)]
-        dy = [[keep.tile([P, 2, HALF], F32, name="dy_%d_%d" % (h, u)) for u in range(2)] for h in range(2)]
-        w_raw = keep.tile([P, PACK, D], F32, name="w_raw")
+        z0 = [keep.tile([P, HALF], F32, name="z0_%d" % j) for j in range(PACK)]
+        dy0 = [keep.tile([P, 2, HALF], F32, name="dy0_%d" % u) for u in range(2)]
+        z1 = [keep.tile([P, PACK, CHUNK], F32, name="z1_%d" % c) for c in range(2)]
+        dy1 = [keep.tile([P, PACK, CHUNK], F32, name="dy1_%d" % c) for c in range(2)]
+        w_raw = [keep.tile([P, PACK, D // 2], F32, name="w_raw_%d" % k) for k in range(2)]
+        w_rows = wm.rearrange("(p j) d -> p j d", j=PACK)
+        identity = keep.tile([P, P], F32, name="identity")
+        make_identity(nc, identity[:])
 
-        def tokens(h):
-            return slice(h * HALF, (h + 1) * HALF)
-
-        nc.sync.dma_start(code1[:], offs)
-        for j in range(PACK):
+        def load_plane(j):
             nc.sync.dma_start(book1[j][:], cb_rows[:, j, :])
-            nc.sync.dma_start(z[0][j][:], z_rows[:, j, tokens(0)])
+            if j == 0:
+                nc.sync.dma_start(code1[:], offs)
+            nc.sync.dma_start(z0[j][:], z_rows[:, j, 0:HALF])
             if j == 0:
                 nc.sync.dma_start(code2[:], offs2)
             nc.sync.dma_start(book2[j][:], cb2_rows[:, j, :])
-            if j % 2 == 1:
-                nc.sync.dma_start(dy[0][j // 2][:], dy_rows[:, j - 1 : j + 1, tokens(0)])
-        for j in range(PACK):
-            nc.sync.dma_start(z[1][j][:], z_rows[:, j, tokens(1)])
-        nc.sync.dma_start(w_raw[:], wm.rearrange("(p j) d -> p j d", j=PACK))
-        for u in range(2):
-            nc.sync.dma_start(dy[1][u][:], dy_rows[:, 2 * u : 2 * u + 2, tokens(1)])
 
-        part = [[keep.tile([P, HALF], F32, name="part_%d_%d" % (h, j)) for j in range(PACK)] for h in range(2)]
-        neg_e = [[keep.tile([P, 2, HALF], F32, name="neg_e_%d_%d" % (h, u)) for u in range(2)] for h in range(2)]
-        g_pairs = [[keep.tile([P, 2, CHUNK * 2], BF16, name="g_pairs_%d_%d" % (h, c)) for c in range(2)] for h in range(2)]
-        g_in = [[keep.tile([P, CHUNK * PACK], BF16, name="g_in_%d_%d" % (h, c), align_bytes=64) for c in range(2)] for h in range(2)]
-        g_codes = [keep.tile([P, HALF], U32, name="g_codes_%d" % h, align_bytes=64) for h in range(2)]
-        g_scales = [keep.tile([P, HALF], U8, name="g_scales_%d" % h, align_bytes=64) for h in range(2)]
-        w_in = keep.tile([P, PACK * D], BF16, name="w_in", align_bytes=64)
+        def chunk_tokens(c):
+            return slice(HALF + c * CHUNK, HALF + (c + 1) * CHUNK)
+
+        load_plane(0)
+        load_plane(1)
+        nc.sync.dma_start(dy0[0][:], dy_rows[:, 0:2, 0:HALF])
+        load_plane(2)
+        nc.sync.dma_start(w_raw[0][:], w_rows[:, :, 0 : D // 2])
+        load_plane(3)
+        nc.sync.dma_start(dy0[1][:], dy_rows[:, 2:4, 0:HALF])
+        nc.sync.dma_start(z1[0][:], z_rows[:, :, chunk_tokens(0)])
+        nc.sync.dma_start(w_raw[1][:], w_rows[:, :, D // 2 : D])
+        nc.sync.dma_start(dy1[0][:], dy_rows[:, :, chunk_tokens(0)])
+        nc.sync.dma_start(z1[1][:], z_rows[:, :, chunk_tokens(1)])
+        nc.sync.dma_start(dy1[1][:], dy_rows[:, :, chunk_tokens(1)])
+
+        g_codes = keep.tile([P, T], U32, name="g_codes", align_bytes=64)
+        g_scales = keep.tile([P, T], U8, name="g_scales", align_bytes=64)
         w_codes = keep.tile([P, D], U32, name="w_codes", align_bytes=64)
         w_scales = keep.tile([P, D], U8, name="w_scales", align_bytes=64)
-        y = [keep.tile([P, PACK, HALF], F32, name="y_%d" % h) for h in range(2)]
-        y_in = [keep.tile([P, HALF * PACK], BF16, name="y_in_%d" % h, align_bytes=64) for h in range(2)]
         y_codes = keep.tile([P, T], U32, name="y_codes", align_bytes=64)
         y_scales = keep.tile([P, T], U8, name="y_scales", align_bytes=64)
 
-        def offsets(code, h, c):
-            first = (h * HALF + c * CHUNK) // GROUP
-            return code[:, first : first + CHUNK // GROUP]
+        def offsets(code, first, last):
+            return code[:, first // GROUP : last // GROUP]
 
-        def look_up_1(h, j, c):
-            cols = slice(c * CHUNK, (c + 1) * CHUNK)
-            nc.vector.tensor_tensor(part[h][j][:, cols], book1[j][:].indirect(offsets(code1, h, c)), z[h][j][:, cols], SUB)
+        def quantise_g(g_in, first, last):
+            nc.vector.quantize_mx(g_codes[:, first:last].bitcast(E5M2), g_scales[:, first:last], g_in[:])
 
-        def look_up_2(h, j, c):
-            cols = slice(c * CHUNK, (c + 1) * CHUNK)
-            nc.vector.tensor_tensor(neg_e[h][j // 2][:, j % 2, cols], book2[j][:].indirect(offsets(code2, h, c)), part[h][j][:, cols], ADD)
+        def multiply_moving(first, tags):
+            banks = []
+            for j in range(PACK):
+                bank = psum.tile([P, HALF], F32, name="y_bank_%d_%d" % (first, j), tag=tags[j])
+                cols = slice(j * P, (j + 1) * P)
+                nc.tensor.matmul_mx(bank[:], lhsT=w_codes[:, cols].bitcast(E4M3), lhsT_scale=w_scales[:, cols],
+                                    rhs=g_codes[:, first : first + HALF].bitcast(E5M2), rhs_scale=g_scales[:, first : first + HALF],
+                                    start=True, stop=True)
+                banks.append(bank)
+            return banks
 
-        def form_g(h, u, c):
-            cols = slice(c * CHUNK, (c + 1) * CHUNK)
+        def weave_y(y_in, y):
+            nc.scalar.copy(
+                y_in[:].rearrange("p (c i j) -> p c j i", i=4, j=PACK),
+                y[:].rearrange("p j (c i) -> p c j i", i=4),
+            )
+
+        def quantise_y(y_in, first, last):
+            nc.vector.quantize_mx(y_codes[:, first:last].bitcast(E4M3), y_scales[:, first:last], y_in[:])
+
+        def store_words(first, last):
+            nc.sync.dma_start(word_rows[:, first:last], y_codes[:, first:last].bitcast(I32))
+
+        def deal_w(k):
+            nc.scalar.copy(
+                w_in[:].rearrange("p (i m j) -> p m j i", i=PACK, j=PACK)[:, k * (P // 2) : (k + 1) * (P // 2), :, :],
+                w_raw[k][:].rearrange("p j (m i) -> p m j i", i=PACK),
+            )
+
+        part0 = [keep.tile([P, HALF], F32, name="part0_%d" % j) for j in range(PACK)]
+        neg_e0 = [keep.tile([P, HALF], F32, name="neg_e0_%d" % j) for j in range(PACK)]
+        neg_dy = [keep.tile([P, 2, HALF], F32, name="neg_dy_%d" % u) for u in range(2)]
+        sums = [psum.tile([P, PACK, P], F32, name="sum_%d" % b, tag="s%d" % b) for b in range(4)]
+        g_rows = [[keep.tile([P, 2 * P], BF16, name="g_rows_%d_%d" % (b, u)) for u in range(2)] for b in range(4)]
+        g_in0 = keep.tile([P, HALF * PACK], BF16, name="g_in0", tag="share_g", align_bytes=64)
+        w_in = keep.tile([P, PACK * D], BF16, name="w_in", tag="share_w", align_bytes=64)
+        for j in range(PACK):
+            u, e = divmod(j, 2)
+            for c in range(2):
+                cols = slice(c * CHUNK, (c + 1) * CHUNK)
+                nc.vector.tensor_tensor(part0[j][:, cols], book1[j][:].indirect(offsets(code1, cols.start, cols.stop)), z0[j][:, cols], SUB)
+            for c in range(2):
+                cols = slice(c * CHUNK, (c + 1) * CHUNK)
+                nc.vector.tensor_tensor(neg_e0[j][:, cols], book2[j][:].indirect(offsets(code2, cols.start, cols.stop)), part0[j][:, cols], ADD)
+            if e == 0:
+                nc.scalar.activation(neg_dy[u][:], dy0[u][:], COPY, scale=-1.0 / BETA)
+            for b in range(4):
+                blk = slice(b * P, (b + 1) * P)
+                nc.tensor.matmul(sums[b][:, j, :], lhsT=neg_dy[u][:, e, blk], rhs=identity[:], start=True, stop=False, is_transpose=True)
+                nc.tensor.matmul(sums[b][:, j, :], lhsT=neg_e0[j][:, blk], rhs=identity[:], start=False, stop=True, is_transpose=True)
+                if e == 1:
+                    nc.scalar.activation(
+                        g_rows[b][u][:].rearrange("t (p e) -> t p e", e=2),
+                        sums[b][:, 2 * u : 2 * u + 2, :].rearrange("t e p -> t p e"),
+                        COPY,
+                        scale=-BETA,
+                    )
+            if j == 1:
+                deal_w(0)
+        deal_w(1)
+        for k in range(2):
+            words = psum.tile([P, 2, 2, P], F32, name="words_%d" % k, tag="w%d" % k)
+            for bb in range(2):
+                for u in range(2):
+                    nc.tensor.transpose(words[:, bb, u, :], g_rows[2 * k + bb][u][:].bitcast(F32), identity[:])
+            nc.scalar.copy(
+                g_in0[:, k * CHUNK * PACK : (k + 1) * CHUNK * PACK].bitcast(F32).rearrange("p (b t u) -> p b t u", b=2, u=2),
+                words[:].rearrange("p b u t -> p b t u"),
+            )
+
+        def local(first, last):
+            c = (first - HALF) // CHUNK
+            return c, slice(first - HALF - c * CHUNK, last - HALF - c * CHUNK)
+
+        def look_up_1(part, j, first, last):
+            c, cols = local(first, last)
+            nc.vector.tensor_tensor(part[:, j, :], book1[j][:].indirect(offsets(code1, first, last)), z1[c][:, j, cols], SUB)
+
+        def look_up_2(neg_e, part, j, first, last):
+            nc.vector.tensor_tensor(neg_e[:, j, :], book2[j][:].indirect(offsets(code2, first, last)), part[:, j, :], ADD)
+
+        def form_g(pairs, neg_e, u, first, last):
+            c, cols = local(first, last)
             nc.vector.scalar_tensor_tensor(
-                g_pairs[h][c][:, u, :].rearrange("p (t e) -> p t e", e=2),
-                neg_e[h][u][:, :, cols].rearrange("p e t -> p t e"),
+                pairs[:, u, :].rearrange("p (t e) -> p t e", e=2),
+                neg_e[:, 2 * u : 2 * u + 2, :].rearrange("p e t -> p t e"),
                 -BETA,
-                dy[h][u][:, :, cols].rearrange("p e t -> p t e"),
+                dy1[c][:, 2 * u : 2 * u + 2, cols].rearrange("p e t -> p t e"),
                 MULT,
                 ADD,
             )
 
-        def weave_g(h, c):
-            nc.scalar.copy(
-                g_in[h][c][:].bitcast(F32).rearrange("p (t u) -> p t u", u=2),
-                g_pairs[h][c][:].bitcast(F32).rearrange("p u t -> p t u"),
+        def weave_g(g_in, pairs):
+            nc.vector.tensor_copy(
+                g_in[:].bitcast(F32).rearrange("p (t u) -> p t u", u=2),
+                pairs[:].bitcast(F32).rearrange("p u t -> p t u"),
             )
 
-        def quantise_g(h, c):
-            cols = slice(c * CHUNK, (c + 1) * CHUNK)
-            nc.vector.quantize_mx(g_codes[h][:, cols].bitcast(E5M2), g_scales[h][:, cols], g_in[h][c][:])
+        def tiles(first, width, part_tag, neg_tag):
+            part = keep.tile([P, PACK, width], F32, name="part_%d" % first, tag=part_tag, align_bytes=64)
+            pairs = keep.tile([P, 2, 2 * width], BF16, name="pairs_%d" % first)
+            g_in = keep.tile([P, width * PACK], BF16, name="g_in_%d" % first, align_bytes=64)
+            return part, pairs, g_in
 
-        def multiply(h):
-            banks = []
-            for j in range(PACK):
-                bank = psum.tile([P, HALF], F32, name="bank_%d_%d" % (h, j))
-                cols = slice(j * P, (j + 1) * P)
-                nc.tensor.matmul_mx(bank[:], lhsT=w_codes[:, cols].bitcast(E4M3), lhsT_scale=w_scales[:, cols],
-                                    rhs=g_codes[h][:].bitcast(E5M2), rhs_scale=g_scales[h][:], start=True, stop=True)
-                banks.append(bank)
-            return banks
+        def multiply_stationary(first, tag):
+            bank = psum.tile([P, D], F32, name="yt_bank_%d" % first, tag=tag)
+            nc.tensor.matmul_mx(bank[:], lhsT=g_codes[:, first : first + P].bitcast(E5M2), lhsT_scale=g_scales[:, first : first + P],
+                                rhs=w_codes[:].bitcast(E4M3), rhs_scale=w_scales[:], start=True, stop=True)
+            return bank
 
-        def weave_y(engine_copy, h, first, last):
-            engine_copy(
-                y_in[h][:, first * PACK : last * PACK].rearrange("p (c i j) -> p c j i", i=4, j=PACK),
-                y[h][:, :, first:last].rearrange("p j (c i) -> p c j i", i=4),
-            )
+        def turn_back(first, bank, tag):
+            y_t = keep.tile([P, D], F32, name="y_t_%d" % first)
+            turned = psum.tile([P, PACK, P], F32, name="turned_%d" % first, tag=tag)
+            for k in range(2):
+                nc.scalar.copy(y_t[:, k * 2 * P : (k + 1) * 2 * P], bank[:, k * 2 * P : (k + 1) * 2 * P])
+                for j in (2 * k, 2 * k + 1):
+                    nc.tensor.transpose(turned[:, j, :], y_t[:, j * P : (j + 1) * P], identity[:])
+            return turned
 
-        def quantise_y(h):
-            nc.vector.quantize_mx(y_codes[:, tokens(h)].bitcast(E4M3), y_scales[:, tokens(h)], y_in[h][:])
-            nc.sync.dma_start(word_rows[:, tokens(h)], y_codes[:, tokens(h)].bitcast(I32))
-
+        A, B6, B7 = 512, 768, 896
+        part_a, pairs_a, g_in_a = tiles(A, CHUNK, "part_a", "")
         for j in range(PACK):
-            for c in range(2):
-                look_up_1(0, j, c)
-            for c in range(2):
-                look_up_2(0, j, c)
-            if j % 2 == 1:
-                for c in range(2):
-                    form_g(0, j // 2, c)
-        for c in range(2):
-            weave_g(0, c)
-        nc.scalar.copy(
-            w_in[:].rearrange("p (i m j) -> p m j i", i=PACK, j=PACK),
-            w_raw[:].rearrange("p j (m i) -> p m j i", i=PACK),
-        )
-
-        for j in range(PACK):
-            look_up_1(1, j, 0)
-        for c in range(2):
-            quantise_g(0, c)
+            look_up_1(part_a, j, A, B6)
         nc.vector.quantize_mx(w_codes[:].bitcast(E4M3), w_scales[:], w_in[:])
-        banks = multiply(0)
+        neg_a = keep.tile([P, PACK, CHUNK], F32, name="neg_a", tag="share_w", align_bytes=64)
         for j in range(PACK):
-            nc.scalar.copy(y[0][:, j, :], banks[j][:])
-        nc.sync.dma_start(y_rows[:, :, tokens(0)], y[0][:])
-        weave_y(nc.scalar.copy, 0, 0, HALF)
-        for j in range(PACK):
-            look_up_2(1, j, 0)
-        for j in range(PACK):
-            look_up_1(1, j, 1)
-            if j % 2 == 1:
-                form_g(1, j // 2, 0)
-        weave_g(1, 0)
-        for j in range(PACK):
-            look_up_2(1, j, 1)
-            if j == 1:
-                quantise_g(1, 0)
-                quantise_y(0)
+            look_up_2(neg_a, part_a, j, A, B6)
             if j == 2:
-                form_g(1, 0, 1)
-        form_g(1, 1, 1)
-        weave_g(1, 1)
-        quantise_g(1, 1)
-        banks = multiply(1)
+                form_g(pairs_a, neg_a, 0, A, B6)
+        quantise_g(g_in0, 0, HALF)
+        banks = multiply_moving(0, ["m0", "m1", "w0", "w1"])
+        y0 = keep.tile([P, PACK, HALF], F32, name="y0")
         for j in range(PACK):
-            if j % 2 == 0:
-                nc.scalar.copy(y[1][:, j, :], banks[j][:])
-            else:
-                nc.vector.tensor_copy(y[1][:, j, :], banks[j][:])
-                nc.sync.dma_start(y_rows[:, j - 1 : j + 1, tokens(1)], y[1][:, j - 1 : j + 1, :])
-        weave_y(nc.scalar.copy, 1, 0, 160)
-        weave_y(nc.vector.tensor_copy, 1, 160, HALF)
-        quantise_y(1)
+            nc.scalar.copy(y0[:, j, :], banks[j][:])
+        nc.sync.dma_start(y_rows[:, :, 0:HALF], y0[:])
+        y_in0 = keep.tile([P, HALF * PACK], BF16, name="y_in0", align_bytes=64)
+        weave_y(y_in0, y0)
+
+        form_g(pairs_a, neg_a, 1, A, B6)
+        part_6, pairs_6, g_in_6 = tiles(B6, P, "share_g", "")
+        for j in range(PACK):
+            look_up_1(part_6, j, B6, B7)
+            if j == 0:
+                weave_g(g_in_a, pairs_a)
+            if j == 1:
+                quantise_g(g_in_a, A, B6)
+        banks = multiply_moving(B6 - HALF, ["s0", "s1", "s2", "s3"])
+        y_a = keep.tile([P, PACK, CHUNK], F32, name="y_a")
+        for j in range(PACK):
+            nc.scalar.copy(y_a[:, j, :], banks[j][:, HALF - CHUNK : HALF])
+        nc.sync.dma_start(y_rows[:, :, A:B6], y_a[:])
+
+        neg_6 = keep.tile([P, PACK, P], F32, name="neg_6")
+        for j in range(PACK):
+            look_up_2(neg_6, part_6, j, B6, B7)
+            if j == 2:
+                form_g(pairs_6, neg_6, 0, B6, B7)
+        part_7, pairs_7, g_in_7 = tiles(B7, P, "part_7", "")
+        for j in range(PACK):
+            look_up_1(part_7, j, B7, T)
+            if j == 0:
+                form_g(pairs_6, neg_6, 1, B6, B7)
+            if j == 1:
+                weave_g(g_in_6, pairs_6)
+            if j == 2:
+                quantise_g(g_in_6, B6, B7)
+        bank_6 = multiply_stationary(B6, "m0")
+        turned_6 = turn_back(B6, bank_6, "m1")
+        y_in_a = keep.tile([P, CHUNK * PACK], BF16, name="y_in_a", align_bytes=64)
+        weave_y(y_in_a, y_a)
+        y_6 = keep.tile([P, PACK, P], F32, name="y_6")
+        nc.scalar.copy(y_6[:], turned_6[:])
+        nc.sync.dma_start(y_rows[:, :, B6:B7], y_6[:])
+
+        neg_7 = keep.tile([P, PACK, P], F32, name="neg_7")
+        for j in range(PACK):
+            look_up_2(neg_7, part_7, j, B7, T)
+            if j == 2:
+                form_g(pairs_7, neg_7, 0, B7, T)
+        form_g(pairs_7, neg_7, 1, B7, T)
+        weave_g(g_in_7, pairs_7)
+        quantise_g(g_in_7, B7, T)
+        bank_7 = multiply_stationary(B7, "w0")
+        turned_7 = turn_back(B7, bank_7, "w1")
+
+        quantise_y(y_in0, 0, HALF)
+        y_in_6 = keep.tile([P, P * PACK], BF16, name="y_in_6", align_bytes=64)
+        nc.vector.tensor_copy(y_in_6[:].rearrange("p (t j) -> p t j", j=PACK), turned_6[:].rearrange("p j t -> p t j"))
+        quantise_y(y_in_a, A, B6)
+        quantise_y(y_in_6, B6, B7)
+        store_words(0, B7)
+        y_in_7 = keep.tile([P, P * PACK], BF16, name="y_in_7", align_bytes=64)
+        nc.vector.tensor_copy(y_in_7[:].rearrange("p (t j) -> p t j", j=PACK), turned_7[:].rearrange("p j t -> p t j"))
+        y_7 = keep.tile([P, PACK, P], F32, name="y_7")
+        nc.scalar.copy(y_7[:], turned_7[:])
+        quantise_y(y_in_7, B7, T)
+        store_words(B7, T)
+        nc.scalar.dma_start(y_rows[:, :, B7:T], y_7[:])
         for q in range(4):
-            engine = nc.scalar if q % 2 == 0 else nc.sync
+            engine = nc.scalar if q % 2 == 1 else nc.sync
             engine.dma_start(scale_rows[4 * q : 4 * q + 4, :], y_scales[32 * q : 32 * q + 4, :].bitcast(I32))

@@ -25,6 +25,9 @@ PACK = 4
 HALF = 512
 CHUNK = 256
 GROUP = 16
+TURNED = 4
+WINDOW1 = 1024
+WINDOW2 = 544
 
 
 def tile_attend_gvq_pl_rs_x_kernel(tc, zT, cb, cb2, dyT, wm, offs, offs2, out_0, out_1, out_2):
@@ -43,41 +46,55 @@ def tile_attend_gvq_pl_rs_x_kernel(tc, zT, cb, cb2, dyT, wm, offs, offs2, out_0,
 
         code1 = keep.tile([P, T // GROUP], U16, name="code1")
         code2 = keep.tile([P, T // GROUP], U16, name="code2")
-        book1 = [keep.tile([P, C], F32, name="book1_%d" % j) for j in range(PACK)]
-        book2 = [keep.tile([P, C], F32, name="book2_%d" % j) for j in range(PACK)]
+        book1 = [keep.tile([P, WINDOW1], F32, name="book1_%d" % j) for j in range(PACK)]
+        book2 = [keep.tile([P, WINDOW2], F32, name="book2_%d" % j) for j in range(PACK)]
         z0 = [keep.tile([P, HALF], F32, name="z0_%d" % j) for j in range(PACK)]
         dy0 = [keep.tile([P, 2, HALF], F32, name="dy0_%d" % u) for u in range(2)]
-        z1 = [keep.tile([P, PACK, CHUNK], F32, name="z1_%d" % c) for c in range(2)]
-        dy1 = [keep.tile([P, PACK, CHUNK], F32, name="dy1_%d" % c) for c in range(2)]
+        z1 = [keep.tile([P, 2, HALF], F32, name="z1_%d" % u) for u in range(2)]
+        dy1 = [keep.tile([P, 2, HALF], F32, name="dy1_%d" % u) for u in range(2)]
         w_raw = [keep.tile([P, PACK, D // 2], F32, name="w_raw_%d" % k) for k in range(2)]
         w_rows = wm.rearrange("(p j) d -> p j d", j=PACK)
         identity = keep.tile([P, P], F32, name="identity")
         make_identity(nc, identity[:])
+        for j in range(PACK):
+            nc.gpsimd.memset(book1[j][:, C:WINDOW1], 0.0)
+            nc.gpsimd.memset(book2[j][:, C:WINDOW2], 0.0)
 
-        def load_plane(j):
-            nc.sync.dma_start(book1[j][:], cb_rows[:, j, :])
+        def load_first(j):
+            nc.sync.dma_start(book1[j][:, 0:C], cb_rows[:, j, :])
             if j == 0:
                 nc.sync.dma_start(code1[:], offs)
             nc.sync.dma_start(z0[j][:], z_rows[:, j, 0:HALF])
+
+        def load_second(j):
             if j == 0:
                 nc.sync.dma_start(code2[:], offs2)
-            nc.sync.dma_start(book2[j][:], cb2_rows[:, j, :])
+            nc.sync.dma_start(book2[j][:, 0:C], cb2_rows[:, j, :])
+
+        def load_dy0(j):
+            nc.sync.dma_start(dy0[j // 2][:, j % 2, :], dy_rows[:, j, 0:HALF])
 
         def chunk_tokens(c):
             return slice(HALF + c * CHUNK, HALF + (c + 1) * CHUNK)
 
-        load_plane(0)
-        load_plane(1)
-        nc.sync.dma_start(dy0[0][:], dy_rows[:, 0:2, 0:HALF])
-        load_plane(2)
+        load_first(0)
+        load_first(1)
+        load_second(0)
+        load_first(2)
+        load_second(1)
+        load_dy0(0)
+        load_first(3)
+        load_dy0(1)
+        load_second(2)
+        load_dy0(2)
+        load_second(3)
+        load_dy0(3)
+        nc.sync.dma_start(z1[0][:], z_rows[:, 0:2, HALF:T])
         nc.sync.dma_start(w_raw[0][:], w_rows[:, :, 0 : D // 2])
-        load_plane(3)
-        nc.sync.dma_start(dy0[1][:], dy_rows[:, 2:4, 0:HALF])
-        nc.sync.dma_start(z1[0][:], z_rows[:, :, chunk_tokens(0)])
+        nc.sync.dma_start(z1[1][:], z_rows[:, 2:4, HALF:T])
         nc.sync.dma_start(w_raw[1][:], w_rows[:, :, D // 2 : D])
-        nc.sync.dma_start(dy1[0][:], dy_rows[:, :, chunk_tokens(0)])
-        nc.sync.dma_start(z1[1][:], z_rows[:, :, chunk_tokens(1)])
-        nc.sync.dma_start(dy1[1][:], dy_rows[:, :, chunk_tokens(1)])
+        nc.sync.dma_start(dy1[0][:], dy_rows[:, 0:2, HALF:T])
+        nc.sync.dma_start(dy1[1][:], dy_rows[:, 2:4, HALF:T])
 
         g_codes = keep.tile([P, T], U32, name="g_codes", align_bytes=64)
         g_scales = keep.tile([P, T], U8, name="g_scales", align_bytes=64)
@@ -90,7 +107,7 @@ def tile_attend_gvq_pl_rs_x_kernel(tc, zT, cb, cb2, dyT, wm, offs, offs2, out_0,
             return code[:, first // GROUP : last // GROUP]
 
         def quantise_g(g_in, first, last):
-            nc.vector.quantize_mx(g_codes[:, first:last].bitcast(E5M2), g_scales[:, first:last], g_in[:])
+            nc.vector.quantize_mx(g_codes[:, first:last].bitcast(E5M2), g_scales[:, first:last], g_in)
 
         def multiply_moving(first, tags):
             banks = []
@@ -110,38 +127,40 @@ def tile_attend_gvq_pl_rs_x_kernel(tc, zT, cb, cb2, dyT, wm, offs, offs2, out_0,
             )
 
         def quantise_y(y_in, first, last):
-            nc.vector.quantize_mx(y_codes[:, first:last].bitcast(E4M3), y_scales[:, first:last], y_in[:])
+            nc.vector.quantize_mx(y_codes[:, first:last].bitcast(E4M3), y_scales[:, first:last], y_in)
 
         def store_words(first, last):
             nc.sync.dma_start(word_rows[:, first:last], y_codes[:, first:last].bitcast(I32))
 
         def deal_w(k):
             nc.scalar.copy(
-                w_in[:].rearrange("p (i m j) -> p m j i", i=PACK, j=PACK)[:, k * (P // 2) : (k + 1) * (P // 2), :, :],
+                w_in.rearrange("p (i m j) -> p m j i", i=PACK, j=PACK)[:, k * (P // 2) : (k + 1) * (P // 2), :, :],
                 w_raw[k][:].rearrange("p j (m i) -> p m j i", i=PACK),
             )
 
+        edge = TURNED * P
         part0 = [keep.tile([P, HALF], F32, name="part0_%d" % j) for j in range(PACK)]
-        neg_e0 = [keep.tile([P, HALF], F32, name="neg_e0_%d" % j) for j in range(PACK)]
-        neg_dy = [keep.tile([P, 2, HALF], F32, name="neg_dy_%d" % u) for u in range(2)]
-        sums = [psum.tile([P, PACK, P], F32, name="sum_%d" % b, tag="s%d" % b) for b in range(4)]
-        g_rows = [[keep.tile([P, 2 * P], BF16, name="g_rows_%d_%d" % (b, u)) for u in range(2)] for b in range(4)]
-        g_in0 = keep.tile([P, HALF * PACK], BF16, name="g_in0", tag="share_g", align_bytes=64)
-        w_in = keep.tile([P, PACK * D], BF16, name="w_in", tag="share_w", align_bytes=64)
-        for j in range(PACK):
+        neg_e0 = [keep.tile([P, 2, HALF], F32, name="neg_e0_%d" % u) for u in range(2)]
+        neg_dy = [keep.tile([P, max(edge, P)], F32, name="neg_dy_%d" % j) for j in range(PACK)]
+        sums = [psum.tile([P, PACK, P], F32, name="sum_%d" % b, tag="s%d" % b) for b in range(TURNED)]
+        g_rows = [[keep.tile([P, 2 * P], BF16, name="g_rows_%d_%d" % (b, u)) for u in range(2)] for b in range(TURNED)]
+        pairs0 = keep.tile([P, 2, 2 * max(HALF - edge, P)], BF16, name="pairs0")
+        shared = keep.tile([P, 2 * HALF + 4 * 384], F32, name="shared", align_bytes=64)
+        g_in0 = shared[:, 0 : 2 * HALF].bitcast(BF16)
+        w_in = shared[:, 2 * HALF : 4 * HALF].bitcast(BF16)
+
+        def first_1(j):
+            nc.vector.tensor_tensor(part0[j][:], book1[j][:].indirect(offsets(code1, 0, HALF)), z0[j][:], SUB)
+
+        def first_2(j):
             u, e = divmod(j, 2)
-            for c in range(2):
-                cols = slice(c * CHUNK, (c + 1) * CHUNK)
-                nc.vector.tensor_tensor(part0[j][:, cols], book1[j][:].indirect(offsets(code1, cols.start, cols.stop)), z0[j][:, cols], SUB)
-            for c in range(2):
-                cols = slice(c * CHUNK, (c + 1) * CHUNK)
-                nc.vector.tensor_tensor(neg_e0[j][:, cols], book2[j][:].indirect(offsets(code2, cols.start, cols.stop)), part0[j][:, cols], ADD)
-            if e == 0:
-                nc.scalar.activation(neg_dy[u][:], dy0[u][:], COPY, scale=-1.0 / BETA)
-            for b in range(4):
+            nc.vector.tensor_tensor(neg_e0[u][:, e, :], book2[j][:].indirect(offsets(code2, 0, HALF)), part0[j][:], ADD)
+            if TURNED:
+                nc.scalar.activation(neg_dy[j][:], dy0[u][:, e, 0:edge], COPY, scale=-1.0 / BETA)
+            for b in range(TURNED):
                 blk = slice(b * P, (b + 1) * P)
-                nc.tensor.matmul(sums[b][:, j, :], lhsT=neg_dy[u][:, e, blk], rhs=identity[:], start=True, stop=False, is_transpose=True)
-                nc.tensor.matmul(sums[b][:, j, :], lhsT=neg_e0[j][:, blk], rhs=identity[:], start=False, stop=True, is_transpose=True)
+                nc.tensor.matmul(sums[b][:, j, :], lhsT=neg_dy[j][:, blk], rhs=identity[:], start=True, stop=False, is_transpose=True)
+                nc.tensor.matmul(sums[b][:, j, :], lhsT=neg_e0[u][:, e, blk], rhs=identity[:], start=False, stop=True, is_transpose=True)
                 if e == 1:
                     nc.scalar.activation(
                         g_rows[b][u][:].rearrange("t (p e) -> t p e", e=2),
@@ -149,52 +168,59 @@ def tile_attend_gvq_pl_rs_x_kernel(tc, zT, cb, cb2, dyT, wm, offs, offs2, out_0,
                         COPY,
                         scale=-BETA,
                     )
-            if j == 1:
-                deal_w(0)
-        deal_w(1)
-        for k in range(2):
-            words = psum.tile([P, 2, 2, P], F32, name="words_%d" % k, tag="w%d" % k)
-            for bb in range(2):
-                for u in range(2):
-                    nc.tensor.transpose(words[:, bb, u, :], g_rows[2 * k + bb][u][:].bitcast(F32), identity[:])
-            nc.scalar.copy(
-                g_in0[:, k * CHUNK * PACK : (k + 1) * CHUNK * PACK].bitcast(F32).rearrange("p (b t u) -> p b t u", b=2, u=2),
-                words[:].rearrange("p b u t -> p b t u"),
-            )
+
+        def first_g(u):
+            if edge < HALF:
+                nc.vector.scalar_tensor_tensor(
+                    pairs0[:, u, :].rearrange("p (t e) -> p t e", e=2),
+                    neg_e0[u][:, :, edge:HALF].rearrange("p e t -> p t e"),
+                    -BETA,
+                    dy0[u][:, :, edge:HALF].rearrange("p e t -> p t e"),
+                    MULT,
+                    ADD,
+                )
+
+        first_1(0)
+        first_1(1)
+        first_2(0)
+        first_1(2)
+        first_2(1)
+        first_1(3)
+        first_g(0)
+        first_2(2)
+        first_2(3)
 
         def local(first, last):
             c = (first - HALF) // CHUNK
             return c, slice(first - HALF - c * CHUNK, last - HALF - c * CHUNK)
 
         def look_up_1(part, j, first, last):
-            c, cols = local(first, last)
-            nc.vector.tensor_tensor(part[:, j, :], book1[j][:].indirect(offsets(code1, first, last)), z1[c][:, j, cols], SUB)
+            nc.vector.tensor_tensor(part, book1[j][:].indirect(offsets(code1, first, last)), z1[j // 2][:, j % 2, first - HALF : last - HALF], SUB)
 
         def look_up_2(neg_e, part, j, first, last):
-            nc.vector.tensor_tensor(neg_e[:, j, :], book2[j][:].indirect(offsets(code2, first, last)), part[:, j, :], ADD)
+            nc.vector.tensor_tensor(neg_e, book2[j][:].indirect(offsets(code2, first, last)), part, ADD)
 
-        def form_g(pairs, neg_e, u, first, last):
-            c, cols = local(first, last)
+        def form_g(out, neg_e, u, first, last):
             nc.vector.scalar_tensor_tensor(
-                pairs[:, u, :].rearrange("p (t e) -> p t e", e=2),
-                neg_e[:, 2 * u : 2 * u + 2, :].rearrange("p e t -> p t e"),
+                out,
+                neg_e.rearrange("p e t -> p t e"),
                 -BETA,
-                dy1[c][:, 2 * u : 2 * u + 2, cols].rearrange("p e t -> p t e"),
+                dy1[u][:, :, first - HALF : last - HALF].rearrange("p e t -> p t e"),
                 MULT,
                 ADD,
             )
 
-        def weave_g(g_in, pairs):
-            nc.vector.tensor_copy(
+        def as_pairs(pairs, u):
+            return pairs[:, u, :].rearrange("p (t e) -> p t e", e=2)
+
+        def in_place(g_in, u):
+            return g_in.rearrange("p (t j) -> p t j", j=PACK)[:, :, 2 * u : 2 * u + 2]
+
+        def weave_g(copy, g_in, pairs):
+            copy(
                 g_in[:].bitcast(F32).rearrange("p (t u) -> p t u", u=2),
                 pairs[:].bitcast(F32).rearrange("p u t -> p t u"),
             )
-
-        def tiles(first, width, part_tag, neg_tag):
-            part = keep.tile([P, PACK, width], F32, name="part_%d" % first, tag=part_tag, align_bytes=64)
-            pairs = keep.tile([P, 2, 2 * width], BF16, name="pairs_%d" % first)
-            g_in = keep.tile([P, width * PACK], BF16, name="g_in_%d" % first, align_bytes=64)
-            return part, pairs, g_in
 
         def multiply_stationary(first, tag):
             bank = psum.tile([P, D], F32, name="yt_bank_%d" % first, tag=tag)
@@ -202,94 +228,101 @@ def tile_attend_gvq_pl_rs_x_kernel(tc, zT, cb, cb2, dyT, wm, offs, offs2, out_0,
                                 rhs=w_codes[:].bitcast(E4M3), rhs_scale=w_scales[:], start=True, stop=True)
             return bank
 
-        def turn_back(first, bank, tag):
-            y_t = keep.tile([P, D], F32, name="y_t_%d" % first)
-            turned = psum.tile([P, PACK, P], F32, name="turned_%d" % first, tag=tag)
-            for k in range(2):
-                nc.scalar.copy(y_t[:, k * 2 * P : (k + 1) * 2 * P], bank[:, k * 2 * P : (k + 1) * 2 * P])
-                for j in (2 * k, 2 * k + 1):
-                    nc.tensor.transpose(turned[:, j, :], y_t[:, j * P : (j + 1) * P], identity[:])
-            return turned
-
-        A, B6, B7 = 512, 768, 896
-        part_a, pairs_a, g_in_a = tiles(A, CHUNK, "part_a", "")
-        for j in range(PACK):
-            look_up_1(part_a, j, A, B6)
-        nc.vector.quantize_mx(w_codes[:].bitcast(E4M3), w_scales[:], w_in[:])
-        neg_a = keep.tile([P, PACK, CHUNK], F32, name="neg_a", tag="share_w", align_bytes=64)
-        for j in range(PACK):
-            look_up_2(neg_a, part_a, j, A, B6)
+        A, B7 = 512, 896
+        MID = B7 - A
+        part_a = keep.tile([P, PACK, MID], F32, name="part_a")
+        neg_a0 = keep.tile([P, 2, MID], F32, name="neg_a0")
+        neg_a1 = shared[:, 2 * HALF : 2 * HALF + 2 * MID].rearrange("p (e x) -> p e x", e=2)
+        pairs_a = shared[:, 2 * HALF + 2 * MID : 2 * HALF + 4 * MID].rearrange("p (u x) -> p u x", u=2)
+        g_in_a = keep.tile([P, 2 * MID], F32, name="g_in_a", align_bytes=64)
+        deal_w(0)
+        for k in range(0, TURNED, 2):
+            words = psum.tile([P, 2, 2, P], F32, name="words_%d" % k, tag="w%d" % (k // 2))
+            for bb in range(2):
+                for u in range(2):
+                    nc.tensor.transpose(words[:, bb, u, :], g_rows[k + bb][u][:].bitcast(F32), identity[:])
+            nc.scalar.copy(
+                shared[:, k * 2 * P : (k + 2) * 2 * P].rearrange("p (b t u) -> p b t u", b=2, u=2),
+                words[:].rearrange("p b u t -> p b t u"),
+            )
+            if k == 0:
+                deal_w(1)
+        for j in range(2):
+            look_up_1(part_a[:, j, :], j, A, B7)
+        for j in range(2):
+            look_up_2(neg_a0[:, j, :], part_a[:, j, :], j, A, B7)
+        for j in range(2, PACK):
+            look_up_1(part_a[:, j, :], j, A, B7)
+        nc.vector.quantize_mx(w_codes[:].bitcast(E4M3), w_scales[:], w_in)
+        nc.vector.quantize_mx(g_codes[:, 0:HALF].bitcast(E5M2), g_scales[:, 0:HALF], g_in0)
+        for j in range(2, PACK):
+            look_up_2(neg_a1[:, j - 2, :], part_a[:, j, :], j, A, B7)
             if j == 2:
-                form_g(pairs_a, neg_a, 0, A, B6)
-        quantise_g(g_in0, 0, HALF)
+                form_g(pairs_a[:, 0, :].bitcast(BF16).rearrange("p (t e) -> p t e", e=2), neg_a0[:], 0, A, B7)
+        form_g(pairs_a[:, 1, :].bitcast(BF16).rearrange("p (t e) -> p t e", e=2), neg_a1, 1, A, B7)
         banks = multiply_moving(0, ["m0", "m1", "w0", "w1"])
-        y0 = keep.tile([P, PACK, HALF], F32, name="y0")
-        for j in range(PACK):
-            nc.scalar.copy(y0[:, j, :], banks[j][:])
-        nc.sync.dma_start(y_rows[:, :, 0:HALF], y0[:])
-        y_in0 = keep.tile([P, HALF * PACK], BF16, name="y_in0", align_bytes=64)
-        weave_y(y_in0, y0)
+        y = keep.tile([P, PACK, B7], F32, name="y")
+        y_in = keep.tile([P, B7 * PACK], BF16, name="y_in", align_bytes=64)
 
-        form_g(pairs_a, neg_a, 1, A, B6)
-        part_6, pairs_6, g_in_6 = tiles(B6, P, "share_g", "")
-        for j in range(PACK):
-            look_up_1(part_6, j, B6, B7)
-            if j == 0:
-                weave_g(g_in_a, pairs_a)
-            if j == 1:
-                quantise_g(g_in_a, A, B6)
-        banks = multiply_moving(B6 - HALF, ["s0", "s1", "s2", "s3"])
-        y_a = keep.tile([P, PACK, CHUNK], F32, name="y_a")
-        for j in range(PACK):
-            nc.scalar.copy(y_a[:, j, :], banks[j][:, HALF - CHUNK : HALF])
-        nc.sync.dma_start(y_rows[:, :, A:B6], y_a[:])
+        def weave(copy, first, last):
+            copy(
+                y_in[:, first * PACK : last * PACK].rearrange("p (c i j) -> p c j i", i=4, j=PACK),
+                y[:, :, first:last].rearrange("p j (c i) -> p c j i", i=4),
+            )
 
-        neg_6 = keep.tile([P, PACK, P], F32, name="neg_6")
         for j in range(PACK):
-            look_up_2(neg_6, part_6, j, B6, B7)
-            if j == 2:
-                form_g(pairs_6, neg_6, 0, B6, B7)
-        part_7, pairs_7, g_in_7 = tiles(B7, P, "part_7", "")
-        for j in range(PACK):
-            look_up_1(part_7, j, B7, T)
-            if j == 0:
-                form_g(pairs_6, neg_6, 1, B6, B7)
-            if j == 1:
-                weave_g(g_in_6, pairs_6)
-            if j == 2:
-                quantise_g(g_in_6, B6, B7)
-        bank_6 = multiply_stationary(B6, "m0")
-        turned_6 = turn_back(B6, bank_6, "m1")
-        y_in_a = keep.tile([P, CHUNK * PACK], BF16, name="y_in_a", align_bytes=64)
-        weave_y(y_in_a, y_a)
-        y_6 = keep.tile([P, PACK, P], F32, name="y_6")
-        nc.scalar.copy(y_6[:], turned_6[:])
-        nc.sync.dma_start(y_rows[:, :, B6:B7], y_6[:])
+            nc.scalar.copy(y[:, j, 0:HALF], banks[j][:])
+            if j % 2 == 1:
+                nc.sync.dma_start(y_rows[:, j - 1 : j + 1, 0:HALF], y[:, j - 1 : j + 1, 0:HALF])
+            if j == 3:
+                nc.scalar.copy(g_in_a[:].rearrange("p (t u) -> p t u", u=2), pairs_a.rearrange("p u t -> p t u"))
+        weave(nc.scalar.copy, 0, 384)
 
+        part_7 = [neg_a0[:, 0, 0:P], part_a[:, 3, 0:P], g_in_a[:, 0:P], g_in_a[:, P : 2 * P]]
         neg_7 = keep.tile([P, PACK, P], F32, name="neg_7")
+        g_in_7 = y_in[:, (HALF - P) * PACK : HALF * PACK]
+        for j in range(2):
+            look_up_1(part_7[j], j, B7, T)
+        for j in range(2):
+            look_up_2(neg_7[:, j, :], part_7[j], j, B7, T)
+        form_g(in_place(g_in_7, 0), neg_7[:, 0:2, :], 0, B7, T)
+        for first, last in ((A, A + CHUNK), (A + CHUNK, B7)):
+            quantise_g(g_in_a[:, 2 * (first - A) : 2 * (last - A)].bitcast(BF16), first, last)
+        banks = multiply_moving(B7 - HALF, ["s0", "s1", "s2", "s3"])
         for j in range(PACK):
-            look_up_2(neg_7, part_7, j, B7, T)
-            if j == 2:
-                form_g(pairs_7, neg_7, 0, B7, T)
-        form_g(pairs_7, neg_7, 1, B7, T)
-        weave_g(g_in_7, pairs_7)
-        quantise_g(g_in_7, B7, T)
-        bank_7 = multiply_stationary(B7, "w0")
-        turned_7 = turn_back(B7, bank_7, "w1")
+            nc.scalar.copy(y[:, j, A:B7], banks[j][:, HALF - MID : HALF])
+            if j % 2 == 1:
+                nc.sync.dma_start(y_rows[:, j - 1 : j + 1, A:B7], y[:, j - 1 : j + 1, A:B7])
 
-        quantise_y(y_in0, 0, HALF)
-        y_in_6 = keep.tile([P, P * PACK], BF16, name="y_in_6", align_bytes=64)
-        nc.vector.tensor_copy(y_in_6[:].rearrange("p (t j) -> p t j", j=PACK), turned_6[:].rearrange("p j t -> p t j"))
-        quantise_y(y_in_a, A, B6)
-        quantise_y(y_in_6, B6, B7)
-        store_words(0, B7)
+        for j in range(2, PACK):
+            look_up_1(part_7[j], j, B7, T)
+        for j in range(2, PACK):
+            look_up_2(neg_7[:, j, :], part_7[j], j, B7, T)
+        form_g(in_place(g_in_7, 1), neg_7[:, 2:4, :], 1, B7, T)
+        quantise_g(g_in_7, B7, T)
+        bank_7 = multiply_stationary(B7, "m0")
+        y_t = keep.tile([P, D], F32, name="y_t")
+        turned = [psum.tile([P, 2, P], F32, name="turned_%d" % u, tag=tag) for u, tag in enumerate(("m1", "w0"))]
+        for u in range(2):
+            nc.scalar.copy(y_t[:, u * 2 * P : (u + 1) * 2 * P], bank_7[:, u * 2 * P : (u + 1) * 2 * P])
+            for e in range(2):
+                nc.tensor.transpose(turned[u][:, e, :], y_t[:, (2 * u + e) * P : (2 * u + e + 1) * P], identity[:])
+        weave(nc.vector.tensor_copy, HALF - P, HALF)
+        quantise_y(y_in[:, 0 : HALF * PACK], 0, HALF)
+        store_words(0, HALF)
+        weave(nc.vector.tensor_copy, A, B7)
+        for first, last in ((A, A + CHUNK), (A + CHUNK, B7)):
+            quantise_y(y_in[:, first * PACK : last * PACK], first, last)
+        store_words(A, B7)
         y_in_7 = keep.tile([P, P * PACK], BF16, name="y_in_7", align_bytes=64)
-        nc.vector.tensor_copy(y_in_7[:].rearrange("p (t j) -> p t j", j=PACK), turned_7[:].rearrange("p j t -> p t j"))
         y_7 = keep.tile([P, PACK, P], F32, name="y_7")
-        nc.scalar.copy(y_7[:], turned_7[:])
-        quantise_y(y_in_7, B7, T)
-        store_words(B7, T)
+        for u in range(2):
+            nc.scalar.copy(y_7[:, 2 * u : 2 * u + 2, :], turned[u][:])
         nc.scalar.dma_start(y_rows[:, :, B7:T], y_7[:])
+        for u in range(2):
+            nc.vector.tensor_copy(in_place(y_in_7[:], u), turned[u][:].rearrange("p e t -> p t e"))
+        quantise_y(y_in_7[:], B7, T)
+        store_words(B7, T)
         for q in range(4):
             engine = nc.scalar if q % 2 == 1 else nc.sync
             engine.dma_start(scale_rows[4 * q : 4 * q + 4, :], y_scales[32 * q : 32 * q + 4, :].bitcast(I32))

@@ -22,12 +22,16 @@ COPY = mybir.ActivationFunctionType.Copy
 
 P = 128
 PACK = 4
-HALF = 512
-CHUNK = 256
-GROUP = 16
-TURNED = 4
-WINDOW1 = 1024
-WINDOW2 = 544
+PAIRS = 2
+PASS = 512
+LIST_ROWS = 16
+MIDDLE = PASS
+LAST = T - P
+MID = LAST - MIDDLE
+MID_PARTS = ((MIDDLE, MIDDLE + 2 * P), (MIDDLE + 2 * P, LAST))
+WINDOW1 = 2 * C
+WINDOW2 = C + 32
+SCALAR_WEAVES = PASS - 16
 
 
 def tile_attend_gvq_pl_rs_x_kernel(tc, zT, cb, cb2, dyT, wm, offs, offs2, out_0, out_1, out_2):
@@ -36,7 +40,8 @@ def tile_attend_gvq_pl_rs_x_kernel(tc, zT, cb, cb2, dyT, wm, offs, offs2, out_0,
     dy_rows = dyT.rearrange("(p j) t -> p j t", j=PACK)
     cb_rows = cb.rearrange("(p j) c -> p j c", j=PACK)
     cb2_rows = cb2.rearrange("(p j) c -> p j c", j=PACK)
-    y_rows = out_0.rearrange("(p j) t -> p j t", j=PACK)
+    w_rows = wm.rearrange("(p j) d -> p j d", j=PACK)
+    y_rows = out_0.rearrange("(p i) t -> p i t", i=PACK)
     word_rows = out_1[0].rearrange("p t l -> p (t l)").bitcast(I32)
     scale_rows = out_2[0].bitcast(I32)
 
@@ -44,57 +49,59 @@ def tile_attend_gvq_pl_rs_x_kernel(tc, zT, cb, cb2, dyT, wm, offs, offs2, out_0,
         keep = ctx.enter_context(tc.tile_pool(name="keep", bufs=1))
         psum = ctx.enter_context(tc.psum_pool(name="psum", bufs=1))
 
-        code1 = keep.tile([P, T // GROUP], U16, name="code1")
-        code2 = keep.tile([P, T // GROUP], U16, name="code2")
+        code1 = keep.tile([P, T // LIST_ROWS], U16, name="code1")
+        code2 = keep.tile([P, T // LIST_ROWS], U16, name="code2")
         book1 = [keep.tile([P, WINDOW1], F32, name="book1_%d" % j) for j in range(PACK)]
         book2 = [keep.tile([P, WINDOW2], F32, name="book2_%d" % j) for j in range(PACK)]
-        z0 = [keep.tile([P, HALF], F32, name="z0_%d" % j) for j in range(PACK)]
-        dy0 = [keep.tile([P, 2, HALF], F32, name="dy0_%d" % u) for u in range(2)]
-        z1 = [keep.tile([P, 2, HALF], F32, name="z1_%d" % u) for u in range(2)]
-        dy1 = [keep.tile([P, 2, HALF], F32, name="dy1_%d" % u) for u in range(2)]
-        w_raw = [keep.tile([P, PACK, D // 2], F32, name="w_raw_%d" % k) for k in range(2)]
-        w_rows = wm.rearrange("(p j) d -> p j d", j=PACK)
+        z_first = [keep.tile([P, PASS], F32, name="z_first_%d" % j) for j in range(PACK)]
+        dy_first = [keep.tile([P, PASS], F32, name="dy_first_%d" % j) for j in range(PACK)]
+        z_rest = [keep.tile([P, 2, T - PASS], F32, name="z_rest_%d" % u) for u in range(PAIRS)]
+        dy_rest = [keep.tile([P, 2, T - PASS], F32, name="dy_rest_%d" % u) for u in range(PAIRS)]
+        w_raw = [keep.tile([P, PACK, D // 2], F32, name="w_raw_%d" % h) for h in range(2)]
         identity = keep.tile([P, P], F32, name="identity")
         make_identity(nc, identity[:])
         for j in range(PACK):
             nc.gpsimd.memset(book1[j][:, C:WINDOW1], 0.0)
             nc.gpsimd.memset(book2[j][:, C:WINDOW2], 0.0)
 
-        def load_first(j):
+        def load_book1_and_z(j):
             nc.sync.dma_start(book1[j][:, 0:C], cb_rows[:, j, :])
             if j == 0:
                 nc.sync.dma_start(code1[:], offs)
-            nc.sync.dma_start(z0[j][:], z_rows[:, j, 0:HALF])
+            nc.sync.dma_start(z_first[j][:], z_rows[:, j, 0:PASS])
 
-        def load_second(j):
+        def load_book2(j):
             if j == 0:
                 nc.sync.dma_start(code2[:], offs2)
             nc.sync.dma_start(book2[j][:, 0:C], cb2_rows[:, j, :])
 
-        def load_dy0(j):
-            nc.sync.dma_start(dy0[j // 2][:, j % 2, :], dy_rows[:, j, 0:HALF])
+        def load_dy_first(j):
+            nc.sync.dma_start(dy_first[j][:], dy_rows[:, j, 0:PASS])
 
-        def chunk_tokens(c):
-            return slice(HALF + c * CHUNK, HALF + (c + 1) * CHUNK)
+        def load_rest(tiles, rows, u):
+            nc.sync.dma_start(tiles[u][:], rows[:, 2 * u : 2 * u + 2, PASS:T])
 
-        load_first(0)
-        load_first(1)
-        load_second(0)
-        load_first(2)
-        load_second(1)
-        load_dy0(0)
-        load_first(3)
-        load_dy0(1)
-        load_second(2)
-        load_dy0(2)
-        load_second(3)
-        load_dy0(3)
-        nc.sync.dma_start(z1[0][:], z_rows[:, 0:2, HALF:T])
-        nc.sync.dma_start(w_raw[0][:], w_rows[:, :, 0 : D // 2])
-        nc.sync.dma_start(z1[1][:], z_rows[:, 2:4, HALF:T])
-        nc.sync.dma_start(w_raw[1][:], w_rows[:, :, D // 2 : D])
-        nc.sync.dma_start(dy1[0][:], dy_rows[:, 0:2, HALF:T])
-        nc.sync.dma_start(dy1[1][:], dy_rows[:, 2:4, HALF:T])
+        def load_w(h):
+            nc.sync.dma_start(w_raw[h][:], w_rows[:, :, h * D // 2 : (h + 1) * D // 2])
+
+        load_book1_and_z(0)
+        load_book1_and_z(1)
+        load_book2(0)
+        load_book1_and_z(2)
+        load_book2(1)
+        load_dy_first(0)
+        load_book1_and_z(3)
+        load_dy_first(1)
+        load_book2(2)
+        load_dy_first(2)
+        load_book2(3)
+        load_rest(z_rest, z_rows, 0)
+        load_dy_first(3)
+        load_w(0)
+        load_rest(z_rest, z_rows, 1)
+        load_w(1)
+        load_rest(dy_rest, dy_rows, 0)
+        load_rest(dy_rest, dy_rows, 1)
 
         g_codes = keep.tile([P, T], U32, name="g_codes", align_bytes=64)
         g_scales = keep.tile([P, T], U8, name="g_scales", align_bytes=64)
@@ -104,27 +111,16 @@ def tile_attend_gvq_pl_rs_x_kernel(tc, zT, cb, cb2, dyT, wm, offs, offs2, out_0,
         y_scales = keep.tile([P, T], U8, name="y_scales", align_bytes=64)
 
         def offsets(code, first, last):
-            return code[:, first // GROUP : last // GROUP]
+            return code[:, first // LIST_ROWS : last // LIST_ROWS]
+
+        def look_up_1(part, j, z, first, last):
+            nc.vector.tensor_tensor(part, book1[j][:].indirect(offsets(code1, first, last)), z, SUB)
+
+        def look_up_2(neg_e, j, part, first, last):
+            nc.vector.tensor_tensor(neg_e, book2[j][:].indirect(offsets(code2, first, last)), part, ADD)
 
         def quantise_g(g_in, first, last):
             nc.vector.quantize_mx(g_codes[:, first:last].bitcast(E5M2), g_scales[:, first:last], g_in)
-
-        def multiply_moving(first, tags):
-            banks = []
-            for j in range(PACK):
-                bank = psum.tile([P, HALF], F32, name="y_bank_%d_%d" % (first, j), tag=tags[j])
-                cols = slice(j * P, (j + 1) * P)
-                nc.tensor.matmul_mx(bank[:], lhsT=w_codes[:, cols].bitcast(E4M3), lhsT_scale=w_scales[:, cols],
-                                    rhs=g_codes[:, first : first + HALF].bitcast(E5M2), rhs_scale=g_scales[:, first : first + HALF],
-                                    start=True, stop=True)
-                banks.append(bank)
-            return banks
-
-        def weave_y(y_in, y):
-            nc.scalar.copy(
-                y_in[:].rearrange("p (c i j) -> p c j i", i=4, j=PACK),
-                y[:].rearrange("p j (c i) -> p c j i", i=4),
-            )
 
         def quantise_y(y_in, first, last):
             nc.vector.quantize_mx(y_codes[:, first:last].bitcast(E4M3), y_scales[:, first:last], y_in)
@@ -132,197 +128,186 @@ def tile_attend_gvq_pl_rs_x_kernel(tc, zT, cb, cb2, dyT, wm, offs, offs2, out_0,
         def store_words(first, last):
             nc.sync.dma_start(word_rows[:, first:last], y_codes[:, first:last].bitcast(I32))
 
-        def deal_w(k):
+        def multiply_window(first, tags):
+            banks = []
+            for i in range(PACK):
+                bank = psum.tile([P, PASS], F32, name="window_%d_%d" % (first, i), tag=tags[i])
+                dealt = slice(i * P, (i + 1) * P)
+                nc.tensor.matmul_mx(
+                    bank[:],
+                    lhsT=w_codes[:, dealt].bitcast(E4M3),
+                    lhsT_scale=w_scales[:, dealt],
+                    rhs=g_codes[:, first : first + PASS].bitcast(E5M2),
+                    rhs_scale=g_scales[:, first : first + PASS],
+                    start=True,
+                    stop=True,
+                )
+                banks.append(bank)
+            return banks
+
+        def pair_of(interleaved, u):
+            return interleaved.rearrange("p (t j) -> p t j", j=PACK)[:, :, 2 * u : 2 * u + 2]
+
+        in_words = 2 * PASS
+        shared = keep.tile([P, 2 * in_words + 2 * MID], F32, name="shared", align_bytes=64)
+        w_in = shared[:, MID : MID + in_words].bitcast(BF16)
+        g_words_first = shared[:, MID + in_words : MID + 2 * in_words]
+        neg_e_mid = [keep.tile([P, 2, MID], F32, name="neg_e_mid_0")[:], shared[:, 0 : 2 * MID].rearrange("p (e t) -> p e t", e=2)]
+        pair_words_mid = shared[:, 2 * in_words : 2 * in_words + 2 * MID].rearrange("p (u t) -> p u t", u=PAIRS)
+
+        def deal_w(h):
             nc.scalar.copy(
-                w_in.rearrange("p (i m j) -> p m j i", i=PACK, j=PACK)[:, k * (P // 2) : (k + 1) * (P // 2), :, :],
-                w_raw[k][:].rearrange("p j (m i) -> p m j i", i=PACK),
+                w_in.rearrange("p (i m j) -> p m j i", i=PACK, j=PACK)[:, h * P // 2 : (h + 1) * P // 2, :, :],
+                w_raw[h][:].rearrange("p j (m i) -> p m j i", i=PACK),
             )
 
-        edge = TURNED * P
-        part0 = [keep.tile([P, HALF], F32, name="part0_%d" % j) for j in range(PACK)]
-        neg_e0 = [keep.tile([P, 2, HALF], F32, name="neg_e0_%d" % u) for u in range(2)]
-        neg_dy = [keep.tile([P, max(edge, P)], F32, name="neg_dy_%d" % j) for j in range(PACK)]
-        sums = [psum.tile([P, PACK, P], F32, name="sum_%d" % b, tag="s%d" % b) for b in range(TURNED)]
-        g_rows = [[keep.tile([P, 2 * P], BF16, name="g_rows_%d_%d" % (b, u)) for u in range(2)] for b in range(TURNED)]
-        pairs0 = keep.tile([P, 2, 2 * max(HALF - edge, P)], BF16, name="pairs0")
-        shared = keep.tile([P, 2 * HALF + 4 * 384], F32, name="shared", align_bytes=64)
-        g_in0 = shared[:, 0 : 2 * HALF].bitcast(BF16)
-        w_in = shared[:, 2 * HALF : 4 * HALF].bitcast(BF16)
+        blocks = PASS // P
+        part_first = [keep.tile([P, PASS], F32, name="part_first_%d" % j) for j in range(PACK)]
+        neg_e_first = [keep.tile([P, PASS], F32, name="neg_e_first_%d" % j) for j in range(PACK)]
+        neg_dy = [keep.tile([P, PASS], F32, name="neg_dy_%d" % j) for j in range(PACK)]
+        sums = [psum.tile([P, PACK, P], F32, name="sum_%d" % b, tag="a%d" % b) for b in range(blocks)]
+        g_rows = [[keep.tile([P, 2 * P], BF16, name="g_rows_%d_%d" % (b, u)) for u in range(PAIRS)] for b in range(blocks)]
 
-        def first_1(j):
-            nc.vector.tensor_tensor(part0[j][:], book1[j][:].indirect(offsets(code1, 0, HALF)), z0[j][:], SUB)
+        def first_part(j):
+            look_up_1(part_first[j][:], j, z_first[j][:], 0, PASS)
 
-        def first_2(j):
-            u, e = divmod(j, 2)
-            nc.vector.tensor_tensor(neg_e0[u][:, e, :], book2[j][:].indirect(offsets(code2, 0, HALF)), part0[j][:], ADD)
-            if TURNED:
-                nc.scalar.activation(neg_dy[j][:], dy0[u][:, e, 0:edge], COPY, scale=-1.0 / BETA)
-            for b in range(TURNED):
-                blk = slice(b * P, (b + 1) * P)
-                nc.tensor.matmul(sums[b][:, j, :], lhsT=neg_dy[j][:, blk], rhs=identity[:], start=True, stop=False, is_transpose=True)
-                nc.tensor.matmul(sums[b][:, j, :], lhsT=neg_e0[u][:, e, blk], rhs=identity[:], start=False, stop=True, is_transpose=True)
-                if e == 1:
+        def first_sum(j):
+            look_up_2(neg_e_first[j][:], j, part_first[j][:], 0, PASS)
+            nc.scalar.activation(neg_dy[j][:], dy_first[j][:], COPY, scale=-1.0 / BETA)
+            for b in range(blocks):
+                tokens = slice(b * P, (b + 1) * P)
+                for k, term in enumerate((neg_dy[j], neg_e_first[j])):
+                    nc.tensor.matmul(sums[b][:, j, :], lhsT=term[:, tokens], rhs=identity[:], start=(k == 0), stop=(k == 1), is_transpose=True)
+                if j % 2 == 1:
                     nc.scalar.activation(
-                        g_rows[b][u][:].rearrange("t (p e) -> t p e", e=2),
-                        sums[b][:, 2 * u : 2 * u + 2, :].rearrange("t e p -> t p e"),
+                        g_rows[b][j // 2][:].rearrange("t (p e) -> t p e", e=2),
+                        sums[b][:, j - 1 : j + 1, :].rearrange("t e p -> t p e"),
                         COPY,
                         scale=-BETA,
                     )
 
-        def first_g(u):
-            if edge < HALF:
-                nc.vector.scalar_tensor_tensor(
-                    pairs0[:, u, :].rearrange("p (t e) -> p t e", e=2),
-                    neg_e0[u][:, :, edge:HALF].rearrange("p e t -> p t e"),
-                    -BETA,
-                    dy0[u][:, :, edge:HALF].rearrange("p e t -> p t e"),
-                    MULT,
-                    ADD,
-                )
+        first_part(0)
+        for j in range(1, PACK):
+            first_part(j)
+            first_sum(j - 1)
+        first_sum(PACK - 1)
 
-        first_1(0)
-        first_1(1)
-        first_2(0)
-        first_1(2)
-        first_2(1)
-        first_1(3)
-        first_g(0)
-        first_2(2)
-        first_2(3)
+        def turn_back_first(h):
+            words = psum.tile([P, 2, PAIRS, P], F32, name="words_%d" % h, tag="b%d" % h)
+            for b in range(2):
+                for u in range(PAIRS):
+                    nc.tensor.transpose(words[:, b, u, :], g_rows[2 * h + b][u][:].bitcast(F32), identity[:])
+            nc.scalar.copy(
+                g_words_first[:, h * PASS : (h + 1) * PASS].rearrange("p (b t u) -> p b t u", b=2, u=PAIRS),
+                words[:].rearrange("p b u t -> p b t u"),
+            )
 
-        def local(first, last):
-            c = (first - HALF) // CHUNK
-            return c, slice(first - HALF - c * CHUNK, last - HALF - c * CHUNK)
+        for h in range(2):
+            deal_w(h)
+            turn_back_first(h)
 
-        def look_up_1(part, j, first, last):
-            nc.vector.tensor_tensor(part, book1[j][:].indirect(offsets(code1, first, last)), z1[j // 2][:, j % 2, first - HALF : last - HALF], SUB)
-
-        def look_up_2(neg_e, part, j, first, last):
-            nc.vector.tensor_tensor(neg_e, book2[j][:].indirect(offsets(code2, first, last)), part, ADD)
+        def z_plane(j, first, last):
+            return z_rest[j // 2][:, j % 2, first - PASS : last - PASS]
 
         def form_g(out, neg_e, u, first, last):
             nc.vector.scalar_tensor_tensor(
                 out,
                 neg_e.rearrange("p e t -> p t e"),
                 -BETA,
-                dy1[u][:, :, first - HALF : last - HALF].rearrange("p e t -> p t e"),
+                dy_rest[u][:, :, first - PASS : last - PASS].rearrange("p e t -> p t e"),
                 MULT,
                 ADD,
             )
 
-        def as_pairs(pairs, u):
-            return pairs[:, u, :].rearrange("p (t e) -> p t e", e=2)
+        def form_g_mid(u):
+            form_g(pair_words_mid[:, u, :].bitcast(BF16).rearrange("p (t e) -> p t e", e=2), neg_e_mid[u], u, MIDDLE, LAST)
 
-        def in_place(g_in, u):
-            return g_in.rearrange("p (t j) -> p t j", j=PACK)[:, :, 2 * u : 2 * u + 2]
-
-        def weave_g(copy, g_in, pairs):
-            copy(
-                g_in[:].bitcast(F32).rearrange("p (t u) -> p t u", u=2),
-                pairs[:].bitcast(F32).rearrange("p u t -> p t u"),
-            )
-
-        def multiply_stationary(first, tag):
-            bank = psum.tile([P, D], F32, name="yt_bank_%d" % first, tag=tag)
-            nc.tensor.matmul_mx(bank[:], lhsT=g_codes[:, first : first + P].bitcast(E5M2), lhsT_scale=g_scales[:, first : first + P],
-                                rhs=w_codes[:].bitcast(E4M3), rhs_scale=w_scales[:], start=True, stop=True)
-            return bank
-
-        A, B7 = 512, 896
-        MID = B7 - A
-        part_a = keep.tile([P, PACK, MID], F32, name="part_a")
-        neg_a0 = keep.tile([P, 2, MID], F32, name="neg_a0")
-        neg_a1 = shared[:, 2 * HALF : 2 * HALF + 2 * MID].rearrange("p (e x) -> p e x", e=2)
-        pairs_a = shared[:, 2 * HALF + 2 * MID : 2 * HALF + 4 * MID].rearrange("p (u x) -> p u x", u=2)
-        g_in_a = keep.tile([P, 2 * MID], F32, name="g_in_a", align_bytes=64)
-        deal_w(0)
-        for k in range(0, TURNED, 2):
-            words = psum.tile([P, 2, 2, P], F32, name="words_%d" % k, tag="w%d" % (k // 2))
-            for bb in range(2):
-                for u in range(2):
-                    nc.tensor.transpose(words[:, bb, u, :], g_rows[k + bb][u][:].bitcast(F32), identity[:])
-            nc.scalar.copy(
-                shared[:, k * 2 * P : (k + 2) * 2 * P].rearrange("p (b t u) -> p b t u", b=2, u=2),
-                words[:].rearrange("p b u t -> p b t u"),
-            )
-            if k == 0:
-                deal_w(1)
-        for j in range(2):
-            look_up_1(part_a[:, j, :], j, A, B7)
-        for j in range(2):
-            look_up_2(neg_a0[:, j, :], part_a[:, j, :], j, A, B7)
-        for j in range(2, PACK):
-            look_up_1(part_a[:, j, :], j, A, B7)
+        part_mid = keep.tile([P, PACK, MID], F32, name="part_mid")
+        g_words_mid = keep.tile([P, PAIRS * MID], F32, name="g_words_mid", align_bytes=64)
+        for j in (0, 1):
+            look_up_1(part_mid[:, j, :], j, z_plane(j, MIDDLE, LAST), MIDDLE, LAST)
+        for j in (0, 1):
+            look_up_2(neg_e_mid[0][:, j, :], j, part_mid[:, j, :], MIDDLE, LAST)
+        for j in (2, 3):
+            look_up_1(part_mid[:, j, :], j, z_plane(j, MIDDLE, LAST), MIDDLE, LAST)
         nc.vector.quantize_mx(w_codes[:].bitcast(E4M3), w_scales[:], w_in)
-        nc.vector.quantize_mx(g_codes[:, 0:HALF].bitcast(E5M2), g_scales[:, 0:HALF], g_in0)
-        for j in range(2, PACK):
-            look_up_2(neg_a1[:, j - 2, :], part_a[:, j, :], j, A, B7)
-            if j == 2:
-                form_g(pairs_a[:, 0, :].bitcast(BF16).rearrange("p (t e) -> p t e", e=2), neg_a0[:], 0, A, B7)
-        form_g(pairs_a[:, 1, :].bitcast(BF16).rearrange("p (t e) -> p t e", e=2), neg_a1, 1, A, B7)
-        banks = multiply_moving(0, ["m0", "m1", "w0", "w1"])
-        y = keep.tile([P, PACK, B7], F32, name="y")
-        y_in = keep.tile([P, B7 * PACK], BF16, name="y_in", align_bytes=64)
+        quantise_g(g_words_first.bitcast(BF16), 0, PASS)
+        look_up_2(neg_e_mid[1][:, 0, :], 2, part_mid[:, 2, :], MIDDLE, LAST)
+        form_g_mid(0)
+        look_up_2(neg_e_mid[1][:, 1, :], 3, part_mid[:, 3, :], MIDDLE, LAST)
+        form_g_mid(1)
 
-        def weave(copy, first, last):
+        y_first = keep.tile([P, PACK, PASS], F32, name="y_first")
+        y_mid = keep.tile([P, PACK, MID], F32, name="y_mid")
+        y_in = keep.tile([P, LAST * PACK], BF16, name="y_in", align_bytes=64)
+
+        def weave_y(copy, first, last, planes):
             copy(
-                y_in[:, first * PACK : last * PACK].rearrange("p (c i j) -> p c j i", i=4, j=PACK),
-                y[:, :, first:last].rearrange("p j (c i) -> p c j i", i=4),
+                y_in[:, first * PACK : last * PACK].rearrange("p (c k i) -> p c i k", k=4, i=PACK),
+                planes.rearrange("p i (c k) -> p c i k", k=4),
             )
 
-        for j in range(PACK):
-            nc.scalar.copy(y[:, j, 0:HALF], banks[j][:])
-            if j % 2 == 1:
-                nc.sync.dma_start(y_rows[:, j - 1 : j + 1, 0:HALF], y[:, j - 1 : j + 1, 0:HALF])
-            if j == 3:
-                nc.scalar.copy(g_in_a[:].rearrange("p (t u) -> p t u", u=2), pairs_a.rearrange("p u t -> p t u"))
-        weave(nc.scalar.copy, 0, 384)
+        banks = multiply_window(0, ("c0", "c1", "b0", "b1"))
+        for i in range(PACK):
+            nc.scalar.copy(y_first[:, i, :], banks[i][:])
+            if i % 2 == 1:
+                nc.sync.dma_start(y_rows[:, i - 1 : i + 1, 0:PASS], y_first[:, i - 1 : i + 1, :])
+        weave_y(nc.scalar.copy, 0, SCALAR_WEAVES, y_first[:, :, 0:SCALAR_WEAVES])
 
-        part_7 = [neg_a0[:, 0, 0:P], part_a[:, 3, 0:P], g_in_a[:, 0:P], g_in_a[:, P : 2 * P]]
-        neg_7 = keep.tile([P, PACK, P], F32, name="neg_7")
-        g_in_7 = y_in[:, (HALF - P) * PACK : HALF * PACK]
-        for j in range(2):
-            look_up_1(part_7[j], j, B7, T)
-        for j in range(2):
-            look_up_2(neg_7[:, j, :], part_7[j], j, B7, T)
-        form_g(in_place(g_in_7, 0), neg_7[:, 0:2, :], 0, B7, T)
-        for first, last in ((A, A + CHUNK), (A + CHUNK, B7)):
-            quantise_g(g_in_a[:, 2 * (first - A) : 2 * (last - A)].bitcast(BF16), first, last)
-        banks = multiply_moving(B7 - HALF, ["s0", "s1", "s2", "s3"])
-        for j in range(PACK):
-            nc.scalar.copy(y[:, j, A:B7], banks[j][:, HALF - MID : HALF])
-            if j % 2 == 1:
-                nc.sync.dma_start(y_rows[:, j - 1 : j + 1, A:B7], y[:, j - 1 : j + 1, A:B7])
+        nc.vector.tensor_copy(g_words_mid[:].rearrange("p (t u) -> p t u", u=PAIRS), pair_words_mid.rearrange("p u t -> p t u"))
+        for first, last in MID_PARTS:
+            quantise_g(g_words_mid[:, PAIRS * (first - MIDDLE) : PAIRS * (last - MIDDLE)].bitcast(BF16), first, last)
+        banks = multiply_window(LAST - PASS, ("a0", "a1", "a2", "a3"))
+        for i in range(PACK):
+            nc.scalar.copy(y_mid[:, i, :], banks[i][:, PASS - MID : PASS])
+            if i % 2 == 1:
+                nc.scalar.dma_start(y_rows[:, i - 1 : i + 1, MIDDLE:LAST], y_mid[:, i - 1 : i + 1, :])
 
-        for j in range(2, PACK):
-            look_up_1(part_7[j], j, B7, T)
-        for j in range(2, PACK):
-            look_up_2(neg_7[:, j, :], part_7[j], j, B7, T)
-        form_g(in_place(g_in_7, 1), neg_7[:, 2:4, :], 1, B7, T)
-        quantise_g(g_in_7, B7, T)
-        bank_7 = multiply_stationary(B7, "m0")
-        y_t = keep.tile([P, D], F32, name="y_t")
-        turned = [psum.tile([P, 2, P], F32, name="turned_%d" % u, tag=tag) for u, tag in enumerate(("m1", "w0"))]
-        for u in range(2):
-            nc.scalar.copy(y_t[:, u * 2 * P : (u + 1) * 2 * P], bank_7[:, u * 2 * P : (u + 1) * 2 * P])
+        part_last = [neg_e_mid[0][:, 0, 0:P], part_mid[:, 3, 0:P], g_words_mid[:, 0:P], g_words_mid[:, P : 2 * P]]
+        neg_e_last = keep.tile([P, PACK, P], F32, name="neg_e_last")
+        g_in_last = y_in[:, SCALAR_WEAVES * PACK : (SCALAR_WEAVES + P) * PACK]
+        for u in range(PAIRS):
+            for j in (2 * u, 2 * u + 1):
+                look_up_1(part_last[j], j, z_plane(j, LAST, T), LAST, T)
+            for j in (2 * u, 2 * u + 1):
+                look_up_2(neg_e_last[:, j, :], j, part_last[j], LAST, T)
+            form_g(pair_of(g_in_last, u), neg_e_last[:, 2 * u : 2 * u + 2, :], u, LAST, T)
+        quantise_g(g_in_last, LAST, T)
+
+        product = psum.tile([P, D], F32, name="product_last", tag="c0")
+        nc.tensor.matmul_mx(
+            product[:],
+            lhsT=g_codes[:, LAST:T].bitcast(E5M2),
+            lhsT_scale=g_scales[:, LAST:T],
+            rhs=w_codes[:].bitcast(E4M3),
+            rhs_scale=w_scales[:],
+            start=True,
+            stop=True,
+        )
+        y_turned = keep.tile([P, D], F32, name="y_turned")
+        turned = [psum.tile([P, 2, P], F32, name="turned_%d" % u, tag=tag) for u, tag in enumerate(("c1", "b0"))]
+        for u in range(PAIRS):
+            nc.scalar.copy(y_turned[:, u * 2 * P : (u + 1) * 2 * P], product[:, u * 2 * P : (u + 1) * 2 * P])
             for e in range(2):
-                nc.tensor.transpose(turned[u][:, e, :], y_t[:, (2 * u + e) * P : (2 * u + e + 1) * P], identity[:])
-        weave(nc.vector.tensor_copy, HALF - P, HALF)
-        quantise_y(y_in[:, 0 : HALF * PACK], 0, HALF)
-        store_words(0, HALF)
-        weave(nc.vector.tensor_copy, A, B7)
-        for first, last in ((A, A + CHUNK), (A + CHUNK, B7)):
+                nc.tensor.transpose(turned[u][:, e, :], y_turned[:, (2 * u + e) * P : (2 * u + e + 1) * P], identity[:])
+
+        weave_y(nc.vector.tensor_copy, SCALAR_WEAVES, PASS, y_first[:, :, SCALAR_WEAVES:PASS])
+        quantise_y(y_in[:, 0 : PASS * PACK], 0, PASS)
+        store_words(0, PASS)
+        weave_y(nc.vector.tensor_copy, MIDDLE, LAST, y_mid[:])
+        for first, last in MID_PARTS:
             quantise_y(y_in[:, first * PACK : last * PACK], first, last)
-        store_words(A, B7)
-        y_in_7 = keep.tile([P, P * PACK], BF16, name="y_in_7", align_bytes=64)
-        y_7 = keep.tile([P, PACK, P], F32, name="y_7")
-        for u in range(2):
-            nc.scalar.copy(y_7[:, 2 * u : 2 * u + 2, :], turned[u][:])
-        nc.scalar.dma_start(y_rows[:, :, B7:T], y_7[:])
-        for u in range(2):
-            nc.vector.tensor_copy(in_place(y_in_7[:], u), turned[u][:].rearrange("p e t -> p t e"))
-        quantise_y(y_in_7[:], B7, T)
-        store_words(B7, T)
+        store_words(MIDDLE, LAST)
+
+        y_last = keep.tile([P, PACK, P], F32, name="y_last")
+        y_in_last = keep.tile([P, P * PACK], BF16, name="y_in_last", align_bytes=64)
+        for u in range(PAIRS):
+            nc.scalar.copy(y_last[:, 2 * u : 2 * u + 2, :], turned[u][:])
+        nc.scalar.dma_start(y_rows[:, :, LAST:T], y_last[:])
+        for u in range(PAIRS):
+            nc.vector.tensor_copy(pair_of(y_in_last[:], u), turned[u][:].rearrange("p e t -> p t e"))
+        quantise_y(y_in_last[:], LAST, T)
+        store_words(LAST, T)
         for q in range(4):
-            engine = nc.scalar if q % 2 == 1 else nc.sync
-            engine.dma_start(scale_rows[4 * q : 4 * q + 4, :], y_scales[32 * q : 32 * q + 4, :].bitcast(I32))
+            queue = nc.scalar if q % 2 == 1 else nc.sync
+            queue.dma_start(scale_rows[4 * q : 4 * q + 4, :], y_scales[32 * q : 32 * q + 4, :].bitcast(I32))

@@ -152,7 +152,8 @@ def tile_attend_gvq_pl_rs_x_kernel(tc, zT, cb, cb2, dyT, wm, offs, offs2, out_0,
         shared = keep.tile([P, 2 * in_words + 2 * MID], F32, name="shared", align_bytes=64)
         w_in = shared[:, MID : MID + in_words].bitcast(BF16)
         g_words_first = shared[:, MID + in_words : MID + 2 * in_words]
-        neg_e_mid = [keep.tile([P, 2, MID], F32, name="neg_e_mid_0")[:], shared[:, 0 : 2 * MID].rearrange("p (e t) -> p e t", e=2)]
+        neg_e_mid_0 = keep.tile([P, 2, MID], F32, name="neg_e_mid_0")
+        neg_e_mid = [neg_e_mid_0[:], shared[:, 0 : 2 * MID].rearrange("p (e t) -> p e t", e=2)]
         pair_words_mid = shared[:, 2 * in_words : 2 * in_words + 2 * MID].rearrange("p (u t) -> p u t", u=PAIRS)
 
         def deal_w(h):
@@ -223,7 +224,6 @@ def tile_attend_gvq_pl_rs_x_kernel(tc, zT, cb, cb2, dyT, wm, offs, offs2, out_0,
             form_g(pair_words_mid[:, u, :].bitcast(BF16).rearrange("p (t e) -> p t e", e=2), neg_e_mid[u], u, MIDDLE, LAST)
 
         part_mid = keep.tile([P, PACK, MID], F32, name="part_mid")
-        g_words_mid = keep.tile([P, PAIRS * MID], F32, name="g_words_mid", align_bytes=64)
         for j in (0, 1):
             look_up_1(part_mid[:, j, :], j, z_plane(j, MIDDLE, LAST), MIDDLE, LAST)
         for j in (0, 1):
@@ -240,6 +240,7 @@ def tile_attend_gvq_pl_rs_x_kernel(tc, zT, cb, cb2, dyT, wm, offs, offs2, out_0,
         y_first = keep.tile([P, PACK, PASS], F32, name="y_first")
         y_mid = keep.tile([P, PACK, MID], F32, name="y_mid")
         y_in = keep.tile([P, LAST * PACK], BF16, name="y_in", align_bytes=64)
+        g_words_mid = y_in[:, MIDDLE * PACK : LAST * PACK].bitcast(F32)
 
         def weave_y(copy, first, last, planes):
             copy(
@@ -254,25 +255,26 @@ def tile_attend_gvq_pl_rs_x_kernel(tc, zT, cb, cb2, dyT, wm, offs, offs2, out_0,
                 nc.sync.dma_start(y_rows[:, i - 1 : i + 1, 0:PASS], y_first[:, i - 1 : i + 1, :])
         weave_y(nc.scalar.copy, 0, SCALAR_WEAVES, y_first[:, :, 0:SCALAR_WEAVES])
 
-        nc.vector.tensor_copy(g_words_mid[:].rearrange("p (t u) -> p t u", u=PAIRS), pair_words_mid.rearrange("p u t -> p t u"))
+        nc.vector.tensor_copy(g_words_mid.rearrange("p (t u) -> p t u", u=PAIRS), pair_words_mid.rearrange("p u t -> p t u"))
         for first, last in MID_PARTS:
             quantise_g(g_words_mid[:, PAIRS * (first - MIDDLE) : PAIRS * (last - MIDDLE)].bitcast(BF16), first, last)
         banks = multiply_window(LAST - PASS, ("a0", "a1", "a2", "a3"))
         for i in range(PACK):
             nc.scalar.copy(y_mid[:, i, :], banks[i][:, PASS - MID : PASS])
             if i % 2 == 1:
-                nc.scalar.dma_start(y_rows[:, i - 1 : i + 1, MIDDLE:LAST], y_mid[:, i - 1 : i + 1, :])
+                nc.sync.dma_start(y_rows[:, i - 1 : i + 1, MIDDLE:LAST], y_mid[:, i - 1 : i + 1, :])
 
-        part_last = [neg_e_mid[0][:, 0, 0:P], part_mid[:, 3, 0:P], g_words_mid[:, 0:P], g_words_mid[:, P : 2 * P]]
+        spare = y_in[:, SCALAR_WEAVES * PACK : (SCALAR_WEAVES + P) * PACK].bitcast(F32)
+        part_last = [neg_e_mid[0][:, 0, 0:P], part_mid[:, 3, 0:P], spare[:, P : 2 * P], spare[:, 0:P]]
         neg_e_last = keep.tile([P, PACK, P], F32, name="neg_e_last")
-        g_in_last = y_in[:, SCALAR_WEAVES * PACK : (SCALAR_WEAVES + P) * PACK]
+        g_in_last = keep.tile([P, P * PACK], BF16, name="g_in_last", align_bytes=64)
         for u in range(PAIRS):
             for j in (2 * u, 2 * u + 1):
                 look_up_1(part_last[j], j, z_plane(j, LAST, T), LAST, T)
             for j in (2 * u, 2 * u + 1):
                 look_up_2(neg_e_last[:, j, :], j, part_last[j], LAST, T)
-            form_g(pair_of(g_in_last, u), neg_e_last[:, 2 * u : 2 * u + 2, :], u, LAST, T)
-        quantise_g(g_in_last, LAST, T)
+            form_g(pair_of(g_in_last[:], u), neg_e_last[:, 2 * u : 2 * u + 2, :], u, LAST, T)
+        quantise_g(g_in_last[:], LAST, T)
 
         product = psum.tile([P, D], F32, name="product_last", tag="c0")
         nc.tensor.matmul_mx(

from contextlib import ExitStack

import concourse.mybir as mybir
from concourse.masks import make_identity

T, C, D, DV = 1024, 512, 512, 512
BETA = 0.25
FLOPS = 2 * T * D * DV

F32 = mybir.dt.float32
BF16 = mybir.dt.bfloat16
I32 = mybir.dt.int32
U32 = mybir.dt.uint32
U16 = mybir.dt.uint16
U8 = mybir.dt.uint8
E4M3 = mybir.dt.float8_e4m3fn_x4
E5M2 = mybir.dt.float8_e5m2_x4
ADD = mybir.AluOpType.add
SUB = mybir.AluOpType.subtract
MULT = mybir.AluOpType.mult
COPY = mybir.ActivationFunctionType.Copy

P = 128
PACK = 4
PAIRS = 2
PASS = 512
LIST_ROWS = 16
MIDDLE = PASS
LAST = T - P
MID = LAST - MIDDLE
MID_PARTS = ((MIDDLE, MIDDLE + 2 * P), (MIDDLE + 2 * P, LAST))
WINDOW1 = 2 * C
WINDOW2 = C + 32
SCALAR_WEAVES = PASS - 16


def tile_attend_gvq_pl_rs_x_kernel(tc, zT, cb, cb2, dyT, wm, offs, offs2, out_0, out_1, out_2):
    nc = tc.nc
    z_rows = zT.rearrange("(p j) t -> p j t", j=PACK)
    dy_rows = dyT.rearrange("(p j) t -> p j t", j=PACK)
    cb_rows = cb.rearrange("(p j) c -> p j c", j=PACK)
    cb2_rows = cb2.rearrange("(p j) c -> p j c", j=PACK)
    w_rows = wm.rearrange("(p j) d -> p j d", j=PACK)
    y_rows = out_0.rearrange("(p i) t -> p i t", i=PACK)
    word_rows = out_1[0].rearrange("p t l -> p (t l)").bitcast(I32)
    scale_rows = out_2[0].bitcast(I32)

    with ExitStack() as ctx:
        keep = ctx.enter_context(tc.tile_pool(name="keep", bufs=1))
        psum = ctx.enter_context(tc.psum_pool(name="psum", bufs=1))

        code1 = keep.tile([P, T // LIST_ROWS], U16, name="code1")
        code2 = keep.tile([P, T // LIST_ROWS], U16, name="code2")
        book1 = [keep.tile([P, WINDOW1], F32, name="book1_%d" % j) for j in range(PACK)]
        book2 = [keep.tile([P, WINDOW2], F32, name="book2_%d" % j) for j in range(PACK)]
        z_first = [keep.tile([P, PASS], F32, name="z_first_%d" % j) for j in range(PACK)]
        dy_first = [keep.tile([P, PASS], F32, name="dy_first_%d" % j) for j in range(PACK)]
        z_rest = [keep.tile([P, 2, T - PASS], F32, name="z_rest_%d" % u) for u in range(PAIRS)]
        dy_rest = [keep.tile([P, 2, T - PASS], F32, name="dy_rest_%d" % u) for u in range(PAIRS)]
        w_raw = [keep.tile([P, PACK, D // 2], F32, name="w_raw_%d" % h) for h in range(2)]
        identity = keep.tile([P, P], F32, name="identity")
        make_identity(nc, identity[:])
        for j in range(PACK):
            nc.gpsimd.memset(book1[j][:, C:WINDOW1], 0.0)
            nc.gpsimd.memset(book2[j][:, C:WINDOW2], 0.0)

        def load_book1_and_z(j):
            nc.sync.dma_start(book1[j][:, 0:C], cb_rows[:, j, :])
            if j == 0:
                nc.sync.dma_start(code1[:], offs)
            nc.sync.dma_start(z_first[j][:], z_rows[:, j, 0:PASS])

        def load_book2(j):
            if j == 0:
                nc.sync.dma_start(code2[:], offs2)
            nc.sync.dma_start(book2[j][:, 0:C], cb2_rows[:, j, :])

        def load_dy_first(j):
            nc.sync.dma_start(dy_first[j][:], dy_rows[:, j, 0:PASS])

        def load_rest(tiles, rows, u):
            nc.sync.dma_start(tiles[u][:], rows[:, 2 * u : 2 * u + 2, PASS:T])

        def load_w(h):
            nc.sync.dma_start(w_raw[h][:], w_rows[:, :, h * D // 2 : (h + 1) * D // 2])

        load_book1_and_z(0)
        load_book1_and_z(1)
        load_book2(0)
        load_book1_and_z(2)
        load_book2(1)
        load_dy_first(0)
        load_book1_and_z(3)
        load_dy_first(1)
        load_book2(2)
        load_dy_first(2)
        load_book2(3)
        load_rest(z_rest, z_rows, 0)
        load_dy_first(3)
        load_w(0)
        load_rest(z_rest, z_rows, 1)
        load_w(1)
        load_rest(dy_rest, dy_rows, 0)
        load_rest(dy_rest, dy_rows, 1)

        g_codes = keep.tile([P, T], U32, name="g_codes", align_bytes=64)
        g_scales = keep.tile([P, T], U8, name="g_scales", align_bytes=64)
        w_codes = keep.tile([P, D], U32, name="w_codes", align_bytes=64)
        w_scales = keep.tile([P, D], U8, name="w_scales", align_bytes=64)
        y_codes = keep.tile([P, T], U32, name="y_codes", align_bytes=64)
        y_scales = keep.tile([P, T], U8, name="y_scales", align_bytes=64)

        def offsets(code, first, last):
            return code[:, first // LIST_ROWS : last // LIST_ROWS]

        def look_up_1(part, j, z, first, last):
            nc.vector.tensor_tensor(part, book1[j][:].indirect(offsets(code1, first, last)), z, SUB)

        def look_up_2(neg_e, j, part, first, last):
            nc.vector.tensor_tensor(neg_e, book2[j][:].indirect(offsets(code2, first, last)), part, ADD)

        def quantise_g(g_in, first, last):
            nc.vector.quantize_mx(g_codes[:, first:last].bitcast(E5M2), g_scales[:, first:last], g_in)

        def quantise_y(y_in, first, last):
            nc.vector.quantize_mx(y_codes[:, first:last].bitcast(E4M3), y_scales[:, first:last], y_in)

        def store_words(first, last):
            nc.sync.dma_start(word_rows[:, first:last], y_codes[:, first:last].bitcast(I32))

        def multiply_window(first, tags):
            banks = []
            for i in range(PACK):
                bank = psum.tile([P, PASS], F32, name="window_%d_%d" % (first, i), tag=tags[i])
                dealt = slice(i * P, (i + 1) * P)
                nc.tensor.matmul_mx(
                    bank[:],
                    lhsT=w_codes[:, dealt].bitcast(E4M3),
                    lhsT_scale=w_scales[:, dealt],
                    rhs=g_codes[:, first : first + PASS].bitcast(E5M2),
                    rhs_scale=g_scales[:, first : first + PASS],
                    start=True,
                    stop=True,
                )
                banks.append(bank)
            return banks

        def pair_of(interleaved, u):
            return interleaved.rearrange("p (t j) -> p t j", j=PACK)[:, :, 2 * u : 2 * u + 2]

        in_words = 2 * PASS
        shared = keep.tile([P, 2 * in_words + 2 * MID], F32, name="shared", align_bytes=64)
        w_in = shared[:, MID : MID + in_words].bitcast(BF16)
        g_words_first = shared[:, MID + in_words : MID + 2 * in_words]
        neg_e_mid_0 = keep.tile([P, 2, MID], F32, name="neg_e_mid_0")
        neg_e_mid = [neg_e_mid_0[:], shared[:, 0 : 2 * MID].rearrange("p (e t) -> p e t", e=2)]
        pair_words_mid = shared[:, 2 * in_words : 2 * in_words + 2 * MID].rearrange("p (u t) -> p u t", u=PAIRS)

        def deal_w(h):
            nc.scalar.copy(
                w_in.rearrange("p (i m j) -> p m j i", i=PACK, j=PACK)[:, h * P // 2 : (h + 1) * P // 2, :, :],
                w_raw[h][:].rearrange("p j (m i) -> p m j i", i=PACK),
            )

        blocks = PASS // P
        part_first = [keep.tile([P, PASS], F32, name="part_first_%d" % j) for j in range(PACK)]
        neg_e_first = [keep.tile([P, PASS], F32, name="neg_e_first_%d" % j) for j in range(PACK)]
        neg_dy = [keep.tile([P, PASS], F32, name="neg_dy_%d" % j) for j in range(PACK)]
        sums = [psum.tile([P, PACK, P], F32, name="sum_%d" % b, tag="a%d" % b) for b in range(blocks)]
        g_rows = [[keep.tile([P, 2 * P], BF16, name="g_rows_%d_%d" % (b, u)) for u in range(PAIRS)] for b in range(blocks)]

        def first_part(j):
            look_up_1(part_first[j][:], j, z_first[j][:], 0, PASS)

        def first_sum(j):
            look_up_2(neg_e_first[j][:], j, part_first[j][:], 0, PASS)
            nc.scalar.activation(neg_dy[j][:], dy_first[j][:], COPY, scale=-1.0 / BETA)
            for b in range(blocks):
                tokens = slice(b * P, (b + 1) * P)
                for k, term in enumerate((neg_dy[j], neg_e_first[j])):
                    nc.tensor.matmul(sums[b][:, j, :], lhsT=term[:, tokens], rhs=identity[:], start=(k == 0), stop=(k == 1), is_transpose=True)
                if j % 2 == 1:
                    nc.scalar.activation(
                        g_rows[b][j // 2][:].rearrange("t (p e) -> t p e", e=2),
                        sums[b][:, j - 1 : j + 1, :].rearrange("t e p -> t p e"),
                        COPY,
                        scale=-BETA,
                    )

        first_part(0)
        for j in range(1, PACK):
            first_part(j)
            first_sum(j - 1)
        first_sum(PACK - 1)

        def turn_back_first(h):
            words = psum.tile([P, 2, PAIRS, P], F32, name="words_%d" % h, tag="b%d" % h)
            for b in range(2):
                for u in range(PAIRS):
                    nc.tensor.transpose(words[:, b, u, :], g_rows[2 * h + b][u][:].bitcast(F32), identity[:])
            nc.scalar.copy(
                g_words_first[:, h * PASS : (h + 1) * PASS].rearrange("p (b t u) -> p b t u", b=2, u=PAIRS),
                words[:].rearrange("p b u t -> p b t u"),
            )

        for h in range(2):
            deal_w(h)
            turn_back_first(h)

        def z_plane(j, first, last):
            return z_rest[j // 2][:, j % 2, first - PASS : last - PASS]

        def form_g(out, neg_e, u, first, last):
            nc.vector.scalar_tensor_tensor(
                out,
                neg_e.rearrange("p e t -> p t e"),
                -BETA,
                dy_rest[u][:, :, first - PASS : last - PASS].rearrange("p e t -> p t e"),
                MULT,
                ADD,
            )

        def form_g_mid(u):
            form_g(pair_words_mid[:, u, :].bitcast(BF16).rearrange("p (t e) -> p t e", e=2), neg_e_mid[u], u, MIDDLE, LAST)

        part_mid = keep.tile([P, PACK, MID], F32, name="part_mid")
        for j in (0, 1):
            look_up_1(part_mid[:, j, :], j, z_plane(j, MIDDLE, LAST), MIDDLE, LAST)
        for j in (0, 1):
            look_up_2(neg_e_mid[0][:, j, :], j, part_mid[:, j, :], MIDDLE, LAST)
        for j in (2, 3):
            look_up_1(part_mid[:, j, :], j, z_plane(j, MIDDLE, LAST), MIDDLE, LAST)
        nc.vector.quantize_mx(w_codes[:].bitcast(E4M3), w_scales[:], w_in)
        quantise_g(g_words_first.bitcast(BF16), 0, PASS)
        look_up_2(neg_e_mid[1][:, 0, :], 2, part_mid[:, 2, :], MIDDLE, LAST)
        form_g_mid(0)
        look_up_2(neg_e_mid[1][:, 1, :], 3, part_mid[:, 3, :], MIDDLE, LAST)
        form_g_mid(1)

        y_first = keep.tile([P, PACK, PASS], F32, name="y_first")
        y_mid = keep.tile([P, PACK, MID], F32, name="y_mid")
        y_in = keep.tile([P, LAST * PACK], BF16, name="y_in", align_bytes=64)
        g_words_mid = y_in[:, MIDDLE * PACK : LAST * PACK].bitcast(F32)

        def weave_y(copy, first, last, planes):
            copy(
                y_in[:, first * PACK : last * PACK].rearrange("p (c k i) -> p c i k", k=4, i=PACK),
                planes.rearrange("p i (c k) -> p c i k", k=4),
            )

        banks = multiply_window(0, ("c0", "c1", "b0", "b1"))
        for i in range(PACK):
            nc.scalar.copy(y_first[:, i, :], banks[i][:])
            if i % 2 == 1:
                nc.sync.dma_start(y_rows[:, i - 1 : i + 1, 0:PASS], y_first[:, i - 1 : i + 1, :])
        weave_y(nc.scalar.copy, 0, SCALAR_WEAVES, y_first[:, :, 0:SCALAR_WEAVES])

        nc.vector.tensor_copy(g_words_mid.rearrange("p (t u) -> p t u", u=PAIRS), pair_words_mid.rearrange("p u t -> p t u"))
        for first, last in MID_PARTS:
            quantise_g(g_words_mid[:, PAIRS * (first - MIDDLE) : PAIRS * (last - MIDDLE)].bitcast(BF16), first, last)
        banks = multiply_window(LAST - PASS, ("a0", "a1", "a2", "a3"))
        for i in range(PACK):
            nc.scalar.copy(y_mid[:, i, :], banks[i][:, PASS - MID : PASS])
            if i % 2 == 1:
                nc.sync.dma_start(y_rows[:, i - 1 : i + 1, MIDDLE:LAST], y_mid[:, i - 1 : i + 1, :])

        spare = y_in[:, SCALAR_WEAVES * PACK : (SCALAR_WEAVES + P) * PACK].bitcast(F32)
        part_last = [neg_e_mid[0][:, 0, 0:P], part_mid[:, 3, 0:P], spare[:, P : 2 * P], spare[:, 0:P]]
        neg_e_last = keep.tile([P, PACK, P], F32, name="neg_e_last")
        g_in_last = keep.tile([P, P * PACK], BF16, name="g_in_last", align_bytes=64)
        for u in range(PAIRS):
            for j in (2 * u, 2 * u + 1):
                look_up_1(part_last[j], j, z_plane(j, LAST, T), LAST, T)
            for j in (2 * u, 2 * u + 1):
                look_up_2(neg_e_last[:, j, :], j, part_last[j], LAST, T)
            form_g(pair_of(g_in_last[:], u), neg_e_last[:, 2 * u : 2 * u + 2, :], u, LAST, T)
        quantise_g(g_in_last[:], LAST, T)

        product = psum.tile([P, D], F32, name="product_last", tag="c0")
        nc.tensor.matmul_mx(
            product[:],
            lhsT=g_codes[:, LAST:T].bitcast(E5M2),
            lhsT_scale=g_scales[:, LAST:T],
            rhs=w_codes[:].bitcast(E4M3),
            rhs_scale=w_scales[:],
            start=True,
            stop=True,
        )
        y_turned = keep.tile([P, D], F32, name="y_turned")
        turned = [psum.tile([P, 2, P], F32, name="turned_%d" % u, tag=tag) for u, tag in enumerate(("c1", "b0"))]
        for u in range(PAIRS):
            nc.scalar.copy(y_turned[:, u * 2 * P : (u + 1) * 2 * P], product[:, u * 2 * P : (u + 1) * 2 * P])
            for e in range(2):
                nc.tensor.transpose(turned[u][:, e, :], y_turned[:, (2 * u + e) * P : (2 * u + e + 1) * P], identity[:])

        weave_y(nc.vector.tensor_copy, SCALAR_WEAVES, PASS, y_first[:, :, SCALAR_WEAVES:PASS])
        quantise_y(y_in[:, 0 : PASS * PACK], 0, PASS)
        store_words(0, PASS)
        weave_y(nc.vector.tensor_copy, MIDDLE, LAST, y_mid[:])
        for first, last in MID_PARTS:
            quantise_y(y_in[:, first * PACK : last * PACK], first, last)
        store_words(MIDDLE, LAST)

        y_last = keep.tile([P, PACK, P], F32, name="y_last")
        y_in_last = keep.tile([P, P * PACK], BF16, name="y_in_last", align_bytes=64)
        for u in range(PAIRS):
            nc.scalar.copy(y_last[:, 2 * u : 2 * u + 2, :], turned[u][:])
        nc.scalar.dma_start(y_rows[:, :, LAST:T], y_last[:])
        for u in range(PAIRS):
            nc.vector.tensor_copy(pair_of(y_in_last[:], u), turned[u][:].rearrange("p e t -> p t e"))
        quantise_y(y_in_last[:], LAST, T)
        store_words(LAST, T)
        for q in range(4):
            queue = nc.scalar if q % 2 == 1 else nc.sync
            queue.dma_start(scale_rows[4 * q : 4 * q + 4, :], y_scales[32 * q : 32 * q + 4, :].bitcast(I32))
